import numpy as np, ml_dtypes
CORES = [16,18,20,22]
N = 4
BF = ml_dtypes.bfloat16
def gentries(a):
    return np.ascontiguousarray(a.reshape(8, 16, -1).transpose(0, 2, 1)).reshape(8, -1)
def gtable(e):
    e = np.asarray(e); return np.ascontiguousarray(e.reshape(8, -1, 16).transpose(0, 2, 1)).reshape(128, -1).astype(np.int32)
V, CAP, RO, DEC = 512, 64, 4, 16
S = N * V; E = 16 * S; D = 16 * N
def level(rng, *shape):
    return (256 * rng.random(shape[:2] + (1,) + shape[3:]) * rng.random(shape)).astype(np.int64)
def parts(rng):
    fan = np.argsort(rng.random((N, 8, E)), axis=-1)
    lo = rng.choice(np.array([0, 32, 96]), (N, 8, 1)); cost = lo + ((256 - lo) * rng.random((N, 8, E))).astype(np.int64)
    th = np.stack([rng.permutation(np.array([120, 250, 500, 900, 1300, 1600, 1800, 2000])) for q in range(N)]) + rng.integers(0, 40, (N, 8))
    x = level(rng, N, 8, 16, V); dv = np.where(rng.random((N, 8, 1, RO, V)) < 0.15, level(rng, N, 8, 16, RO, V), 0)
    return x, fan, cost, th, dv
def pack(x, fan, cost, th, dv):
    return {"x0": np.ascontiguousarray(x.reshape(N, 128, V)).astype(np.int32), "fan": np.stack([gtable(a) for a in fan]), "cost": np.ascontiguousarray(cost).astype(np.int32),
            "th": np.ascontiguousarray(np.repeat(th, 16, axis=1)[:, :, None]).astype(np.int32), "drv": np.ascontiguousarray(dv.reshape(N, 128, RO * V)).astype(np.int32)}
def setup_inputs(rng):
    return pack(*parts(rng))
def setup_inputs_room(rng):
    x, fan, cost, th, dv = parts(rng); th = rng.integers(200, 1501, (N, 8)); dv[:, :, :, 0] = 0
    for q in range(N):
        for g in range(8):
            o = rng.permutation(V); t = int(th[q, g]); n = int(rng.choice(np.array([0, 1, CAP - 1, CAP, CAP + 1, V])))
            if q == 0: n = (CAP, CAP + 1, V, CAP - 1, 1, 0, CAP, CAP + 1)[g]
            x[q, g][:, o[:n]] = DEC + (t + 15) // 16 + rng.integers(0, 100, (16, n))
            x[q, g][:, o[n:]] = rng.integers(0, DEC + (t - 1) // 16 + 1, (16, V - n))
    return pack(x, fan, cost, th, dv)
def setup_inputs_ties(rng):
    x, fan, cost, th, dv = parts(rng); th = rng.choice(np.array([1, 2, 15, 16, 17, 255, 1000, 3000]), (N, 8))
    share = np.where(np.arange(8) % 2 == 0, 0.7, 0.1)[None, :, None, None]
    goal = th[:, :, None, None] - 1 + np.where(rng.random((N, 8, 1, V)) < share, rng.integers(1, 3, (N, 8, 1, V)), 0)
    m = goal // 16; y = m + (np.arange(16)[:, None] < goal % 16)
    d = ((np.minimum(m, 254 - DEC - m) + 1) * rng.random((N, 8, 8, V))).astype(np.int64)
    y[:, :, :8] += d; y[:, :, 8:] -= d
    x = np.where(y > 0, y + DEC, rng.integers(0, DEC + 1, y.shape)); dv[:, :, :, 0] = 0
    th[:, 0] = 16 * DEC; th[:, 1] = 16 * DEC + 1
    x[:, :2] = rng.integers(RO * DEC + 1, 256, (N, 2, 16, V)); cost[:, :2] = 255; dv[:, :2] = 0
    x[:, 7] = 0; dv[:, 7] = 0; cost[:, 7] = rng.integers(254, 256, (N, E))
    for q in range(N):
        t = (4080, 4079, 4077, 2049)[q % 4]; th[q, 7] = t; o = rng.permutation(V)[:CAP]
        w = np.repeat(np.array([t - 1, t, 4080]), [CAP // 2, CAP // 4, CAP - CAP // 2 - CAP // 4])
        dv[q, 7][:, 0][:, o] = w // 16 + (np.arange(16)[:, None] < w % 16)
    return pack(x, fan, cost, th, dv)
def setup_inputs_alike(rng):
    x, fan, cost, th, dv = parts(rng); ar = np.arange(E); s = ar // 16; i = ar % 16
    fan[:, 0] = ar; fan[:, 1] = ar[::-1]; fan[:, 2] = (16 * (s // V) + i) * V + s % V
    for q in range(N): fan[q, 3] = (16 * rng.permutation(S)[:, None] + np.arange(16)).reshape(-1)
    fan[:, 5] = fan[0, 5].copy()
    cost[:, ::2] = rng.choice(np.array([0, 1, 254, 255]), (N, 4, E))
    c = cost[:, 2].reshape(N, D, V).copy(); h = c[:, :, ::2].shape[2]
    c[:, :D - 4, ::2] = rng.integers(254, 256, (N, D - 4, h)); c[:, D - 4:, ::2] = rng.integers(0, 2, (N, 4, h))
    cost[:, 2] = c.reshape(N, E); dv[:, 2, :, :, 0] = 0
    x = rng.choice(np.array([0, DEC - 1, DEC, DEC + 1, 128, 255]), (N, 8, 16, V)); x[..., 0] = 255; x[..., V - 1] = 255
    th = rng.choice(np.array([1, 16, 300, 600]), (N, 8)); th[:, 0] = 1; th[N - 1, 7] = 600
    return pack(x, fan, cost, th, dv)
def setup_inputs_quiet(rng):
    x, fan, cost, th, dv = parts(rng); x = np.minimum(x, 254); dv = np.minimum(dv, 254); h = rng.permutation(8); q = rng.permutation(N)
    th[q[0]] = 1; th[:, h[1]] = 1; th[q[1]] = 4080; th[q[1], h[2]] = 1; th[:, h[0]] = 4080
    x[:, h[1]] = 0; dv[:, h[1]] = 0; dv[q[0], h[1], :, 0, V - 1] = 254
    a = int(h[3]); x[:, a] = 0; dv[:, a, :, :2] = 0
    dv[:, a, :, 2] = np.where(rng.random((N, 1, V)) < 0.3, rng.integers(130, 255, (N, 16, V)), 0)
    b = int(h[4]); x[:, b] = 0; dv[:, b] = 0; cost[:, b] = rng.integers(200, 256, (N, E))
    th[:, b] = rng.integers(1000, 1601, N); th[q[1], b] = 4080; k = max(RO - 4, 0)
    for r in range(N):
        n = int(rng.integers(CAP // 2, CAP + 1)); o = rng.permutation(V)[:n]
        dv[r, b][:, k][:, o] = rng.integers(100, 121, (16, n)); dv[r, b][:, k + 1][:, o] = rng.integers(230, 255, (16, n))
    return pack(x, fan, cost, th, dv)
def setup_inputs_spread(rng):
    x, fan, cost, th, dv = parts(rng)
    x = np.minimum((np.exp2(8 * rng.random((N, 8, 1, V))) * rng.random((N, 8, 16, V))).astype(np.int64), 255)
    w = np.exp2(8 * rng.random((N, 8, E))); cost = np.minimum(np.where(rng.random((N, 8, E)) < 0.5, w - 1, 256 - w).astype(np.int64), 255)
    th = np.minimum(np.maximum(np.exp2(12 * rng.random((N, 8))).astype(np.int64), 1), 4080)
    v = np.minimum((np.exp2(8 * rng.random((N, 8, 1, RO, V))) * rng.random((N, 8, 16, RO, V))).astype(np.int64), 255)
    dv = np.where(rng.random((N, 8, 1, RO, V)) < 0.5 * rng.random((N, 8, 1, RO, 1)), v, 0)
    return pack(x, fan, cost, th, dv)
def check_inputs(d):
    bad = []
    for k, lo, hi in (("x0", 0, 255), ("fan", 0, E - 1), ("cost", 0, 255), ("th", 1, 4080), ("drv", 0, 255)):
        if np.min(d[k]) < lo or np.max(d[k]) > hi: bad.append("range of " + k)
    if not all(np.array_equal(np.sort(gentries(a), axis=1), np.tile(np.arange(E), (8, 1))) for a in d["fan"]): bad.append("every slot once in fan")
    t = d["th"].reshape(-1, 16)
    if np.any(t != t[:, :1]): bad.append("th alike in a group")
    return bad
def reference(x0, fan, cost, th, drv):
    x = x0.astype(np.int64).reshape(N, 8, 16, V); t = th.astype(np.int64).reshape(N, 8, 16)[:, :, :1]; dv = drv.astype(np.int64).reshape(N, 8, 16, RO, V)
    c = cost.astype(np.int16).reshape(N, 8, 1, D, V)
    fl = np.stack([gentries(a) for a in fan]).astype(np.int64).reshape(N, 8, S, 16)
    slots = np.zeros((N, 8, 16, E), np.int16); last = np.zeros((N, 8, 16, V), np.int64)
    for k in range(RO):
        best = np.stack([np.max(slots[r].reshape(8, 16, D, V) - c[r], axis=2) for r in range(N)]).astype(np.int64)
        x = np.maximum(np.maximum(x - DEC, dv[:, :, :, k]), np.maximum(best, 0))
        changed = np.add.reduce(np.abs(x - last), axis=2) >= t
        h = changed.astype(np.int64); sent = changed & (np.add.accumulate(h, axis=2) - h < CAP)
        last = np.where(sent[:, :, None, :], x, last)
        for g in range(8):
            s = np.flatnonzero(sent[:, g].reshape(-1))
            col = x[:, g].transpose(1, 0, 2).reshape(16, S)[:, s].astype(np.int16)
            for r in range(N):
                slots[r, g][:, fl[r, g][s]] = col[:, :, None]
    return {"yx": x.reshape(N, 128, V).astype(np.float32), "yl": last.reshape(N, 128, V).astype(np.float32)}

@@ -1,0 +1,576 @@
+import math
+from concourse.bass import DstId, RemoteDMATransfer
+from concourse.mybir import AluOpType, ActivationFunctionType
+
+V, CAP, RO, DEC, NR = 512, 64, 4, 16, 4
+E = 32768
+SEG = 33
+HALF = SEG * V
+WN = 2 * HALF
+WA, WB = 448, 1600
+ZP = 1024
+ZH = 14
+ZG = (2048, 2048, 2048, 2048, 2048)
+Z1 = 2048
+Z2 = 4096
+N2 = 3
+OWN1 = 16
+CH = 128
+SOW = CH * SEG
+LN2 = math.log(2.0)
+
+SCRATCH = {
+    "W": ("sbuf", [128, WN], "bfloat16"), "CT": ("sbuf", [128, E], "bfloat16"),
+    "SO": ("sbuf", [128, 2 * SOW], "bfloat16"),
+    "fanb": ("sbuf", [128, 2048], "int32"), "cA": ("sbuf", [128, WA], "int32"), "cB": ("sbuf", [128, WB], "int32"),
+    "xi": ("sbuf", [128, V], "int32"), "d0": ("sbuf", [128, V], "int32"), "dr": ("sbuf", [128, 3 * V], "int32"),
+    "thi": ("sbuf", [128, 1], "int32"), "thf": ("sbuf", [128, 1], "float32"), "thS": ("sbuf", [128, V], "float32"),
+    "VS0": ("sbuf", [128, 3072], "bfloat16"), "VS1": ("sbuf", [128, 3072], "bfloat16"),
+    "VO": ("sbuf", [128, 1024], "bfloat16"),
+    "GC": ("sbuf", [128, 4096], "bfloat16"), "GV": ("sbuf", [128, 4096], "bfloat16"),
+    "kf": ("sbuf", [128, V], "bfloat16"), "line": ("sbuf", [128, V], "bfloat16"),
+    "m16": ("sbuf", [128, 128], "bfloat16"), "mm": ("sbuf", [128, 128], "bfloat16"),
+    "Bm": ("sbuf", [128, 128], "bfloat16"), "B2": ("sbuf", [128, 128], "bfloat16"), "NB": ("sbuf", [128, 128], "bfloat16"),
+    "Im": ("sbuf", [128, 128], "bfloat16"), "N16": ("sbuf", [128, 128], "bfloat16"), "NI": ("sbuf", [128, 128], "bfloat16"),
+    "pi": ("sbuf", [128, 4], "int32"), "pf": ("sbuf", [128, 4], "float32"),
+    "oh": ("sbuf", [128, 16], "float32"), "jf": ("sbuf", [128, 8], "float32"),
+    "St": ("sbuf", [128, V], "bfloat16"), "Ls": ("sbuf", [128, V], "bfloat16"), "iS0": ("sbuf", [128, V], "bfloat16"),
+    "xs": ("sbuf", [128, V], "bfloat16"), "mx": ("sbuf", [128, V], "bfloat16"), "ch": ("sbuf", [128, V], "bfloat16"),
+    "ff": ("sbuf", [128, V], "bfloat16"), "xa": ("sbuf", [128, V], "bfloat16"), "xb": ("sbuf", [128, V], "bfloat16"),
+    "dS": ("sbuf", [128, V], "bfloat16"), "acc": ("sbuf", [128, 1024], "float32"),
+    "U": ("sbuf", [128, 4], "uint16"), "ido": ("sbuf", [128, 4], "uint16"),
+    "id0": ("sbuf", [128, 16], "uint16"), "id1": ("sbuf", [128, 16], "uint16"), "id2": ("sbuf", [128, 16], "uint16"),
+    "Eo": ("sbuf", [128, 192], "int32"), "Er": ("sbuf", [128, 576], "int32"),
+    "Jb": ("sbuf", [128, 192], "bfloat16"), "ki": ("sbuf", [128, 32], "int32"), "ku": ("sbuf", [128, 32], "uint16"),
+    "Po": ("sbuf", [128, 128], "float32"), "Pr": ("sbuf", [128, 384], "float32"),
+    "Uo": ("sbuf", [128, 192], "uint16"), "Ur": ("sbuf", [128, 576], "uint16"),
+    "sm": ("sbuf", [128, 256], "bfloat16"), "sf": ("sbuf", [128, 192], "float32"),
+    "xo": ("sbuf", [128, V], "float32"), "lo": ("sbuf", [128, V], "float32"),
+    "pS": ("psum", [128, 512], "float32"), "pX": ("psum", [128, 512], "float32"),
+    "pR0": ("psum", [128, 1024], "float32"), "pR1": ("psum", [128, 2048], "float32"),
+}
+PART = {"Sel": ("GC", 0, 2048), "cm": ("GC", 2048, 1024), "junk": ("GC", 3072, 2 * V),
+        "bA": ("GV", 1024, WA), "bB": ("GV", 1024 + WA, WB)}
+POOL = {"v": 44, "s": 30, "t": 16, "g": 10, "y": 12}
+SEMAPHORES = ([q + str(i) for q in POOL for i in range(POOL[q])] + ["ids%d" % t for t in range(3)]
+              + ["val%d_%d" % (t, d) for t in range(3) for d in range(3)] + ["li%d" % t for t in range(3)]
+              + ["lv%d" % t for t in range(3)] + ["zin", "zout", "zarr", "rep"])
+A = AluOpType
+F = ActivationFunctionType
+
+
+def R(name, lo, hi, step=1):
+    if name in PART:
+        return ("R", PART[name][0], PART[name][1] + lo, PART[name][1] + hi, step)
+    return ("R", name, lo, hi, step)
+
+
+def whole(name):
+    return R(name, 0, PART[name][2] if name in PART else SCRATCH[name][1][1])
+
+
+def X(win, off):
+    return ("X", win, off)
+
+
+def helper_of(core, T, topo):
+    free = [c for c in topo.cores_of(core) if T.rank_of(c) is None]
+    out = {}
+    for r in T.cores:
+        out[r] = [c for c in free if topo.die(c) == topo.die(r) and c not in out.values()][0]
+    return out
+
+
+def rank_program(g, core, T, topo):
+    rank = T.rank_of(core)
+    if rank is not None:
+        main_program(g, core, rank, T, topo)
+    elif topo.chip(core) == topo.chip(T.cores[0]):
+        for r, h in helper_of(core, T, topo).items():
+            if h == core:
+                helper_program(g, core, r, T, topo)
+
+
+def helper_program(g, core, dst, T, topo):
+    n = len(topo.engines(core, dst))
+    rid, pid = topo.addr(dst)[:2]
+    g.wait_ge(T.sem.zin, len(topo.engines(dst, core)))
+    g.remote_dma_fused([RemoteDMATransfer(
+        dst_ids=[DstId(rid=rid, pnc=pid) for k in range(ZH)], dma_engine_mask=topo.mask(core, dst), remote_sem=T.sem.zarr,
+        srcs=[T.W[:, 0:ZP]], dsts=[T.W[:, WN - (k + 1) * ZP:WN - k * ZP] for k in range(ZH)])], local_sem=T.sem.zout)
+    g.wait_ge(T.sem.zout, n)
+
+
+def main_program(g, core, rank, T, topo):
+    Q = {"v": g.vector, "s": g.scalar, "t": g.tensor, "g": g, "y": g.sync}
+    ops = []
+    acc = {}
+    group = [None, None]
+
+    def together(q, calls, name=None):
+        group[0], group[1] = name or len(ops), q
+        for c in calls:
+            pass
+        group[0] = group[1] = None
+
+    def ap(a):
+        if isinstance(a, tuple) and a[0] == "R":
+            return T[a[1]][:, a[2]:a[3]] if a[4] == 1 else T[a[1]][:, a[2]:a[3]:a[4]]
+        if isinstance(a, tuple) and a[0] == "X":
+            return ap(a[1]).indirect(ap(a[2]))
+        return a
+
+    def record(q, fn, reads, writes, dma=False, fixed=None, after=()):
+        me = len(ops)
+        deps = set(after)
+        grp = group[0] if q == group[1] else None
+        touch = [(r, False) for r in reads] + [(r, True) for r in writes]
+        for r, wr in touch:
+            name, lo, hi = r[1:4]
+            ps = SCRATCH[name][0] == "psum"
+            for (l2, h2, o2, w2) in acc.get(name, []):
+                if ps and ops[o2]["q"] != q:
+                    if l2 // 512 <= (hi - 1) // 512 and lo // 512 <= (h2 - 1) // 512:
+                        deps.add(o2)
+                elif grp is not None and ops[o2]["group"] == grp:
+                    continue
+                elif l2 < hi and lo < h2 and (w2 or wr) and not (ps and q == "t"):
+                    deps.add(o2)
+        for r, wr in touch:
+            acc.setdefault(r[1], []).append((r[2], r[3], me, wr))
+        ops.append({"q": q, "fn": fn, "deps": deps, "dma": dma, "fixed": fixed, "group": grp})
+        return me
+
+    def call(q, fn, *args, **kw):
+        reads, writes = [], []
+        for i, a in enumerate(list(args) + [kw[k] for k in kw if k != "accum_out"]):
+            if isinstance(a, tuple) and a[0] == "R":
+                (writes if i == 0 else reads).append(a)
+            elif isinstance(a, tuple) and a[0] == "X":
+                (writes if i == 0 else reads).append(a[1])
+                reads.append(a[2])
+        if "accum_out" in kw:
+            writes.append(kw["accum_out"])
+        return record(q, lambda: fn(*[ap(a) for a in args], **{k: ap(kw[k]) for k in kw}), reads, writes)
+
+    def ts(out, in0, s1, op0, s2=None, op1=None):
+        if op1 is None:
+            return call("v", g.vector.tensor_scalar, out, in0, s1, None, op0)
+        return call("v", g.vector.tensor_scalar, out, in0, s1, s2, op0, op1)
+
+    def tt(out, in0, in1, op):
+        return call("v", g.vector.tensor_tensor, out, in0, in1, op)
+
+    def cp(out, in_):
+        return call("v", g.vector.tensor_copy, out, in_)
+
+    def scan(out, d0, d1, first, op0, op1):
+        return call("v", g.vector.tensor_tensor_scan, out, d0, d1, first, op0, op1)
+
+    def act(out, in_, func, **kw):
+        return call("s", g.scalar.activation, out, in_, func, **kw)
+
+    def mm(out, lhsT, rhs, start, stop):
+        return call("t", g.tensor.matmul, out, lhsT, rhs, start, stop)
+
+    def iota(out, pattern, base, cm):
+        if SCRATCH[out[1]][2] == "int32":
+            return call("g", g.iota, out, pattern, base, cm)
+        return call("g", g.iota, out, pattern, base, cm, allow_small_or_imprecise_dtypes=True)
+
+    def load(q, out, src, after=()):
+        return record(q, lambda: Q[q].dma_start(ap(out), src), [], [out], dma=True, after=after)
+
+    def store(q, dst, src):
+        return record(q, lambda: Q[q].dma_start(dst, ap(src)), [src], [], dma=True)
+
+    def arrival(sem, count, writes):
+        return record(None, None, [], writes, dma=True, fixed=(sem, count))
+
+    def peers_of(r):
+        c = T.cores[r]
+        return sorted([q for q in range(NR) if q != r], key=lambda q: (topo.die(T.cores[q]) != topo.die(c), q ^ r))
+    peers = peers_of(rank)
+    slot = {q: peers_of(q).index(rank) for q in peers}
+    mask = topo.mask(core, T.cores[peers[0]])
+    neng = len(topo.engines(core, T.cores[peers[0]]))
+    helper = helper_of(core, T, topo)[core]
+
+    zend = WN - ZH * ZP - sum(ZG)
+    zpos = [ZP, zend]
+
+    def zero_v(n):
+        together("v", (call("v", g.vector.memset, R("W", a, a + n), 0.0) for a in zpos[:1]), "zv")
+        zpos[0] += n
+
+    def zero_g(n):
+        together("g", (iota(R("W", a, a + n), [[0, n]], 0, 0) for a in zpos[1:]), "zg")
+        zpos[1] += n
+
+    lB = load("s", whole("cB"), T.cost[:, 16 * WA:E])
+    load("y", whole("xi"), T.x0[:])
+    load("y", whole("d0"), T.drv[:, 0:V])
+    load("y", whole("thi"), T.th[:])
+
+    call("v", g.vector.memset, R("W", 0, ZP), 0.0)
+    iota(R("pi", 0, 1), [[0, 1]], 0, 1)
+    iota(whole("kf"), [[0, V // 16], [1, 16]], 0, 0)
+    hr, hp = topo.addr(helper)[:2]
+    record("g", lambda: g.remote_dma(T.W[:, 0:ZP], T.W[:, 0:ZP], T.sem.zin, T.sem.zout, hp, hr, topo.mask(core, helper)),
+           [R("W", 0, ZP)], [], dma=True, fixed=("zout", len(topo.engines(core, helper))))
+    arrival("zarr", ZH * len(topo.engines(helper, core)), [R("W", WN - ZH * ZP, WN)])
+    load("y", whole("cA"), T.cost[:, 0:16 * WA], after=(lB,))
+    load("y", whole("fanb"), T.fan[:])
+    iota(whole("m16"), [[1, 8], [0, 16]], 0, 0)
+    iota(whole("mm"), [[1, 128]], 0, 0)
+    iota(whole("line"), [[1, V]], CAP + 1 - V, 0)
+    iota(whole("Jb"), [[0, 3], [1, 64]], 0, 0)
+    iota(whole("ki"), [[1, 16], [256, 2]], 0, 0)
+    zero_g(ZG[0])
+    zero_g(ZG[1])
+
+    act(whole("St"), whole("kf"), F.Exp, bias=-64 * LN2, scale=8 * LN2)
+    act(whole("pS"), whole("St"), F.Copy)
+    act(whole("Ls"), whole("St"), F.Copy)
+    act(whole("iS0"), whole("kf"), F.Exp, scale=-8 * LN2)
+
+    ts(R("pi", 1, 2), R("pi", 0, 1), 15, A.bitwise_and)
+    ts(R("pi", 2, 3), R("pi", 0, 1), 4, A.arith_shift_right)
+    zero_v(512)
+    cp(R("pf", 0, 3), R("pi", 0, 3))
+    ts(R("pf", 3, 4), R("pi", 1, 2), 0.5, A.add)
+    zero_v(512)
+    ts(whole("oh"), R("kf", 0, 16), R("pf", 1, 2), A.is_equal)
+    ts(R("jf", 0, 4), R("kf", 0, 4), 16.0, A.mult, R("pf", 3, 4), A.add)
+    ts(whole("Bm"), whole("m16"), R("pf", 2, 3), A.is_equal)
+    ts(whole("B2"), whole("m16"), R("pf", 2, 3), A.is_equal, 2.0, A.mult)
+    ts(whole("NB"), whole("m16"), R("pf", 2, 3), A.is_equal, -1.0, A.mult)
+    for h in (0, 8):
+        together("v", (ts(R("Sel", 128 * i, 128 * i + 128), whole("Bm"), R("oh", i, i + 1), A.mult) for i in range(h, h + 8)))
+    ts(whole("Im"), whole("mm"), R("pf", 0, 1), A.is_equal)
+    ts(whole("N16"), whole("mm"), R("pf", 0, 1), A.is_equal, -float(DEC), A.mult)
+
+    def convert(name, w):
+        for a in range(0, w, 512):
+            b = min(a + 512, w)
+            tt(R("b" + name, a, b), R("c" + name, a, b), R("pS", 0, b - a), A.mult)
+
+    piece = [16 * WA, 0, 0]
+    pending = []
+
+    def select(pr, p0, n):
+        a = piece[0]
+        b = piece[0] = min(a + n, E)
+        c = a
+        group[0], group[1] = len(ops), "t"
+        while c < b:
+            i, o = divmod(c - 16 * WA, WB)
+            w = min(WB - o, 512 - (c - a) % 512, b - c)
+            mm(R(pr, p0 + c - a, p0 + c - a + w), R("Sel", 128 * i, 128 * i + 128), R("bB", o, o + w), True, True)
+            c += w
+        group[0] = group[1] = None
+        return R("CT", a, b), R(pr, p0, p0 + b - a)
+
+    def spread_s(n):
+        for j in range(n):
+            if piece[0] < E:
+                piece[1] += 1
+                act(*select("pR1", 1024 * (piece[1] % 2), 1024), F.Copy)
+
+    def fill_v():
+        if piece[0] < E:
+            piece[2] += 1
+            pending.append(select("pR0", 512 * (piece[2] % 2), 512))
+
+    def spread_v():
+        if pending:
+            cp(*pending.pop(0))
+            fill_v()
+
+    def choose(gap=None):
+        scan(whole("ff"), whole("ch"), whole("line"), 0.0, A.add, A.max)
+        for c in (0, 1):
+            ts(R("cm", V * c, V * c + V), whole("ff"), R("jf", c, c + 1), A.is_le, 2.0, A.mult)
+        for c in (2, 3):
+            act(R("junk", V * (c - 2), V * (c - 1)), whole("ff"), F.Sign, bias=R("jf", c, c + 1), scale=-1.0,
+                accum_out=R("acc", 256 * c + 255, 256 * c + 256))
+        for c in (0, 1):
+            scan(R("acc", 256 * c, 256 * c + 256), R("cm", V * c, V * c + 256), R("cm", V * c + 256, V * c + V),
+                 -float(V), A.add, A.add)
+        if gap:
+            gap()
+        ts(whole("U"), R("acc", 255, 1024, 256), 0.5, A.mult, V / 2.0, A.add)
+
+    def lists(ids, n, e, p, u, px):
+        yield cp(R(e, 0, n), X(whole("fanb"), ids))
+        yield cp(R(u, 2 * n, 3 * n), R(e, 0, n))
+        yield ts(R(e, n, 2 * n), R(e, 0, n), 10, A.arith_shift_right)
+        yield ts(R(e, 2 * n, 3 * n), R(e, 0, n), 15, A.bitwise_and)
+        yield ts(R("pX", px, px + n), R(e, n, 2 * n), 1.0 / SEG - 1024, A.mult)
+        yield tt(R(p, n, 2 * n), R(e, 2 * n, 3 * n), R("pX", 256, 256 + n), A.add)
+        yield tt(R(p, 0, n), R(e, 0, n), R("pX", px, px + n), A.add)
+        yield ts(R(u, n, 2 * n), R(p, n, 2 * n), float(CAP), A.mult)
+        yield ts(R(u, 0, n), R(p, 0, n), float(SEG), A.mult, 0.25, A.add)
+
+    def values():
+        U = whole("U")
+        yield cp(R("sm", 0, 64), X(whole("Ls"), U))
+        yield tt(R("sm", 64, 128), X(whole("xs"), U), R("sm", 0, 64), A.subtract)
+        yield tt(R("sm", 128, 192), X(whole("ch"), U), R("sm", 64, 128), A.mult)
+        yield tt(R("sm", 192, 256), R("sm", 128, 192), R("sm", 0, 64), A.add)
+        yield tt(R("VO", 0, 64), X(whole("iS0"), U), R("sm", 192, 256), A.mult)
+        yield together("v", (ts(R("VO", 64 * k, 64 * k + 64), R("VO", 0, 64), 2.0 ** (8 * k), A.mult) for k in (1, 2, 3)))
+        yield together("v", (ts(R("VO", 256 * k, 256 * k + 256), R("VO", 0, 256), 2.0 ** (32 * k), A.mult) for k in (1, 2, 3)))
+
+    def send_ids(t):
+        ts(whole("ido"), R("acc", 255, 1024, 256), 0.5, A.mult, V / 2.0 + V * rank, A.add)
+        idt = "id%d" % t
+        tr = RemoteDMATransfer(
+            dst_ids=[DstId(rid=topo.addr(T.cores[q])[0], pnc=topo.addr(T.cores[q])[1]) for q in peers],
+            dma_engine_mask=mask, remote_sem=T.sem["ids%d" % t], srcs=[T.ido[:]],
+            dsts=[T[idt][:, 4 * slot[q]:4 * slot[q] + 4] for q in peers])
+        record("g", lambda: g.remote_dma_fused([tr], local_sem=T.sem["li%d" % t]), [whole("ido")], [], dma=True,
+               fixed=("li%d" % t, neng))
+        arrival("ids%d" % t, 3 * neng, [R(idt, 0, 12)])
+
+    def send_values(t):
+        vs = "VS%d" % (t % 2)
+        for q in peers:
+            rid, pid = topo.addr(T.cores[q])[:2]
+            record("g", (lambda q=q, rid=rid, pid=pid: g.remote_dma(
+                T[vs][:, 1024 * slot[q]:1024 * slot[q] + 1024], T.VO[:], T.sem["val%d_%d" % (t, slot[q])],
+                T.sem["lv%d" % t], pid, rid, mask)), [whole("VO")], [], dma=True, fixed=("lv%d" % t, 3 * neng))
+        for d in range(3):
+            arrival("val%d_%d" % (t, d), neng, [R(vs, 1024 * d, 1024 * d + 1024)])
+
+    def cost_gather(u, n, a, b, at):
+        act(R("GC", at, at + 16 * (b - a)), X(whole("CT"), R(u, 2 * n + a, 2 * n + b)), F.Identity, scale=-1.0)
+
+    def value_gather(win, u, n, a, b, at):
+        act(R("GV", at, at + 16 * (b - a)), X(win, R(u, n + a, n + b)), F.Identity)
+
+    def own_lists(t):
+        a, b = lists(whole("ido"), 64, "Eo", "Po", "Uo", 0), values()
+        for i, who in enumerate("ababababababaaba"):
+            next(a if who == "a" else b)
+            if t and i == 2:
+                cost_gather("Uo", 64, 0, 64, 0)
+        send_values(t)
+        cp(X(whole("Ls"), whole("U")), R("sm", 192, 256))
+
+    def remote_lists(t):
+        for c in lists(R("id%d" % t, 0, 12), 192, "Er", "Pr", "Ur", 64):
+            pass
+
+    def scatter(u, a, b, at):
+        w = 16 * (b - a)
+        tt(X(whole("W"), R(u, a, b)), R("GC", at, at + w), R("GV", at, at + w), A.add)
+
+    def ahead(t):
+        if t < RO - 1:
+            together("s", (act(R("dS", k, V, 16), X(R("dr", V * t, V * t + V), R("ku", 2 * k, 2 * k + 2)), F.Identity,
+                               bias=2.0 ** (8 * k - 64), scale=2.0 ** (8 * k - 64)) for k in range(16)))
+        else:
+            tt(whole("xo"), whole("Ls"), whole("pS"), A.mult)
+            act(whole("lo"), whole("xo"), F.Identity, bias=-1.0)
+
+    def remote_items(t):
+        vs = "VS%d" % (t % 2)
+        for a, b in ((0, 64), (64, 128), (128, 160), (160, 192)):
+            at, d = 1024 + 16 * a, a // 64
+            cost_gather("Ur", 192, a, b, at)
+            value_gather(R(vs, 1024 * d, 1024 * d + 1024), "Ur", 192, a, b, at)
+            scatter("Ur", a, b, at)
+        if t < RO - 2:
+            ahead(t + 1)
+
+    def cells(half, a, b):
+        return R("W", half * HALF + SEG * a + SEG - 1, half * HALF + SEG * b, SEG)
+
+    convert("B", WB)
+    spread_s(2)
+    zero_v(Z1)
+    cp(whole("thf"), whole("thi"))
+    ts(whole("pX"), whole("xi"), -float(DEC), A.add)
+    tt(whole("mx"), whole("pX"), whole("d0"), A.max)
+    spread_s(1)
+    mm(whole("pX"), whole("Bm"), whole("mx"), True, True)
+    ts(whole("xa"), whole("mx"), 1.0, A.add)
+    tt(whole("xs"), whole("xa"), whole("pS"), A.mult)
+    spread_s(1)
+    ts(whole("ch"), whole("pX"), whole("thf"), A.is_ge)
+    choose(lambda: convert("A", WA))
+    first = record("y", lambda: g.sync.dma_start(T.CT[0:128:16, 0:16 * WA], ap(whole("bA"))), [whole("bA")], [], dma=True)
+    act(R("pX", 256, 448), whole("Jb"), F.Copy, scale=1.0 / CAP)
+    spread_s(2)
+    send_ids(0)
+    zero_g(ZG[2])
+    load("y", R("dr", 0, V), T.drv[:, V:2 * V])
+    for r in range(1, 16):
+        copied = record("y", (lambda r=r: g.sync.dma_start(T.CT[r:128:16, 0:16 * WA], T.CT[0:128:16, 0:16 * WA])),
+                        [], [], dma=True, fixed=("rep", 16 * 15), after=(first,))
+    load("y", R("dr", V, 3 * V), T.drv[:, 2 * V:RO * V])
+    ts(whole("xa"), whole("mx"), 1.0 - DEC, A.add)
+    ts(R("jf", 4, 5), R("pi", 1, 2), 16.0, A.mult)
+    ts(whole("NI"), whole("mm"), R("pf", 0, 1), A.is_equal, -1.0, A.mult)
+    ts(whole("thS"), whole("St"), whole("thf"), A.mult)
+    ts(whole("ku"), whole("ki"), R("jf", 4, 5), A.add)
+    zero_v(Z2)
+    spread_s(2)
+    own_lists(0)
+    cp(R("GV", 0, 1024), X(whole("VO"), R("Uo", 64, 128)))
+    for n in ZG[3:]:
+        zero_g(n)
+    spread_s(4)
+    zero_v(zend - zpos[0])
+    spread_s(N2)
+    fill_v()
+    fill_v()
+    remote_lists(0)
+    ts(whole("xb"), R("dr", 0, V), 1.0, A.add)
+    spread_s(1)
+    while piece[0] < E or pending:
+        spread_v()
+        spread_v()
+        spread_s(1)
+    record("s", None, [], [], after=(copied,))
+    cost_gather("Uo", 64, 0, 32, 0)
+    cost_gather("Uo", 64, 32, 64, 512)
+    tt(cells(0, 0, V), whole("xa"), whole("pS"), A.mult)
+    tt(cells(1, 0, V), whole("xb"), whole("pS"), A.mult)
+    scatter("Uo", 0, 32, 0)
+    scatter("Uo", 32, 64, 512)
+    remote_items(0)
+
+    def chunk_tail(c, last):
+        a, b = CH * c, CH * c + CH
+        so = (c % 2) * SOW
+        view = R("SO", so + SEG - 1, so + SOW, SEG)
+        if c == 3:
+            tt(R("mx", a, b), view, R("Ls", a, b), A.max)
+        act(R("xs", a, b), view, F.Copy)
+        if c == 3:
+            sm = R("pR0", 512, 512 + CH)
+            mm(sm, whole("NB"), R("Ls", a, b), True, False)
+            mm(sm, whole("NB"), R("xs", a, b), False, False)
+            mm(sm, whole("B2"), R("mx", a, b), False, True)
+        else:
+            df = R("pR1", 512 * c + CH, 512 * c + 2 * CH)
+            mm(df, whole("NI"), R("Ls", a, b), True, False)
+            mm(df, whole("Im"), R("xs", a, b), False, True)
+            act(R("mx", a, b), df, F.Abs)
+            mm(R("pR0", a, b), whole("Bm"), R("mx", a, b), True, True)
+        if last:
+            tt(R("acc", a, b), view, R("pS", a, b), A.mult)
+            act(R("xo", a, b), R("acc", a, b), F.Identity, bias=-1.0)
+
+    def chunk_cells(c):
+        a, b = CH * c, CH * c + CH
+        p0 = 512 * c
+        mm(R("pR1", p0, p0 + CH), whole("Im"), R("xs", a, b), True, False)
+        mm(R("pR1", p0, p0 + CH), whole("N16"), R("St", a, b), False, True)
+        act(cells(0, a, b), R("pR1", p0, p0 + CH), F.Copy)
+        act(cells(1, a, b), R("dS", a, b), F.Copy)
+
+    for t in range(1, RO):
+        last = t == RO - 1
+        for c in range(4):
+            for k in range(8):
+                a = SEG * (CH * c + 16 * k)
+                so = (c % 2) * SOW + 16 * SEG * k
+                together("v", (scan(R("SO", so, so + 16 * SEG), R("W", a, a + 16 * SEG),
+                                    R("W", HALF + a, HALF + a + 16 * SEG), 0.0, A.max, A.max) for j in (0,)), ("scan", t, c))
+                if k == 0 and c > 0:
+                    chunk_tail(c - 1, last)
+                    if not last:
+                        chunk_cells(c - 1)
+                    if t == RO - 2 and c == 1:
+                        act(whole("xb"), whole("kf"), F.Exp, bias=64 * LN2, scale=-8 * LN2)
+                        act(whole("pS"), whole("xb"), F.Copy)
+        chunk_tail(3, last)
+        tt(R("ch", 0, 3 * CH), R("pR0", 0, 3 * CH), R("thS", 0, 3 * CH), A.is_ge)
+        tt(R("ch", 3 * CH, V), R("pR0", 512, 512 + CH), R("thS", 3 * CH, V), A.is_ge)
+        if last:
+            ox = store("y", T.yx[:], whole("xo"))
+        choose()
+        if last:
+            U = whole("U")
+            cp(R("sf", 0, 64), X(whole("lo"), U))
+            tt(R("sf", 64, 128), X(whole("xo"), U), R("sf", 0, 64), A.subtract)
+            tt(R("sf", 128, 192), X(whole("ch"), U), R("sf", 64, 128), A.mult)
+            tt(X(whole("lo"), U), R("sf", 128, 192), R("sf", 0, 64), A.add)
+            ol = store("y", T.yl[:], whole("lo"))
+            record("y", None, [], [], after=(ox, ol))
+        else:
+            send_ids(t)
+            chunk_cells(3)
+            own_lists(t)
+            value_gather(whole("VO"), "Uo", 64, 0, OWN1, 0)
+            value_gather(whole("VO"), "Uo", 64, OWN1, 64, 16 * OWN1)
+            if t == RO - 2:
+                ahead(t + 1)
+            scatter("Uo", 0, OWN1, 0)
+            remote_lists(t)
+            scatter("Uo", OWN1, 64, 16 * OWN1)
+            remote_items(t)
+
+    known = {q: set() for q in Q}
+    snap = {}
+    members = {}
+    for i, o in enumerate(ops):
+        members.setdefault(o["group"], []).append(i)
+    needed = set()
+    for i, o in enumerate(ops):
+        q = o["q"]
+        if q is None:
+            snap[i] = set()
+            continue
+        waits = []
+        for d in sorted(o["deps"], reverse=True):
+            if d not in known[q]:
+                waits.append(d)
+                known[q] |= snap[d] | {d}
+                if ops[d]["fixed"] is not None:
+                    known[q] |= {j for j in range(i) if ops[j]["fixed"] == ops[d]["fixed"]}
+                if ops[d]["group"] is not None:
+                    for j in members[ops[d]["group"]]:
+                        known[q] |= snap[j] | {j}
+                        needed.add(j)
+        o["waits"] = waits
+        needed.update(waits)
+        snap[i] = set(known[q])
+    event = {}
+    pool = {q: [[q + str(k), 0, None] for k in range(POOL[q])] for q in POOL}
+    turn = {q: 0 for q in POOL}
+    waited = set()
+    for i, o in enumerate(ops):
+        q = o["q"]
+        if o["fixed"] is not None:
+            event[i] = o["fixed"]
+        if q is None:
+            continue
+        for ev in sorted({event[d] for d in o["waits"]}):
+            Q[q].wait_ge(T.sem[ev[0]], ev[1])
+            waited.add(ev)
+        if o["fn"] is None:
+            continue
+        ins = o["fn"]()
+        if o["fixed"] is not None:
+            if o["fixed"][0] == "rep":
+                ins.then_inc(T.sem.rep, 16)
+        elif i in event:
+            ins.then_inc(T.sem[event[i][0]], 1)
+        elif i in needed:
+            n = len(pool[q])
+            k = [(turn[q] + j) % n for j in range(n)
+                 if pool[q][(turn[q] + j) % n][2] is None or pool[q][(turn[q] + j) % n][2] in snap[i]][0]
+            turn[q] = k + 1
+            inc = 16 if o["dma"] else 1
+            mine = [i] if o["group"] is None else members[o["group"]]
+            pool[q][k][1] += inc * len(mine)
+            pool[q][k][2] = mine[-1]
+            ins.then_inc(T.sem[pool[q][k][0]], inc)
+            for j in mine:
+                event[j] = (pool[q][k][0], pool[q][k][1])
+    for ev in sorted({o["fixed"] for o in ops if o["fixed"] is not None} - waited):
+        g.wait_ge(T.sem[ev[0]], ev[1])

@@ -7,36 +7,43 @@ E = 32768
 SEG = 33
 HALF = SEG * V
 WN = 2 * HALF
-WA, WB = 448, 1600
+WA = 640
+NS = (3, 3, 4)
+BW = (256, 512, 640)
+WB = sum(BW)
 ZP = 1024
-ZH = 14
-ZG = (2048, 2048, 2048, 2048, 2048)
-Z1 = 2048
-Z2 = 4096
-N2 = 3
-OWN1 = 16
-CH = 128
-SOW = CH * SEG
+KS = 1
+O1 = 0
+ORDER = "ababababbabbaaaa"
+ZH = 13
+ZG = (2048, 2048, 2048, 1536)
+ZV = (1536, 1024, 2048, 2048)
+RING = 256
+F0, F1 = 384, 448
+FW = V - F0
+BIG = 2.0 ** 70
 LN2 = math.log(2.0)
 
 SCRATCH = {
     "W": ("sbuf", [128, WN], "bfloat16"), "CT": ("sbuf", [128, E], "bfloat16"),
-    "SO": ("sbuf", [128, 2 * SOW], "bfloat16"),
+    "SO": ("sbuf", [128, RING * SEG], "bfloat16"),
     "fanb": ("sbuf", [128, 2048], "int32"), "cA": ("sbuf", [128, WA], "int32"), "cB": ("sbuf", [128, WB], "int32"),
     "xi": ("sbuf", [128, V], "int32"), "d0": ("sbuf", [128, V], "int32"), "dr": ("sbuf", [128, 3 * V], "int32"),
-    "thi": ("sbuf", [128, 1], "int32"), "thf": ("sbuf", [128, 1], "float32"), "thS": ("sbuf", [128, V], "float32"),
+    "thi": ("sbuf", [128, 1], "int32"), "thf": ("sbuf", [128, 1], "float32"),
     "VS0": ("sbuf", [128, 3072], "bfloat16"), "VS1": ("sbuf", [128, 3072], "bfloat16"),
     "VO": ("sbuf", [128, 1024], "bfloat16"),
     "GC": ("sbuf", [128, 4096], "bfloat16"), "GV": ("sbuf", [128, 4096], "bfloat16"),
-    "kf": ("sbuf", [128, V], "bfloat16"), "line": ("sbuf", [128, V], "bfloat16"),
+    "kf": ("sbuf", [128, 256], "bfloat16"), "line": ("sbuf", [128, V], "bfloat16"),
     "m16": ("sbuf", [128, 128], "bfloat16"), "mm": ("sbuf", [128, 128], "bfloat16"),
     "Bm": ("sbuf", [128, 128], "bfloat16"), "B2": ("sbuf", [128, 128], "bfloat16"), "NB": ("sbuf", [128, 128], "bfloat16"),
     "Im": ("sbuf", [128, 128], "bfloat16"), "N16": ("sbuf", [128, 128], "bfloat16"), "NI": ("sbuf", [128, 128], "bfloat16"),
-    "pi": ("sbuf", [128, 4], "int32"), "pf": ("sbuf", [128, 4], "float32"),
-    "oh": ("sbuf", [128, 16], "float32"), "jf": ("sbuf", [128, 8], "float32"),
+    "TW": ("sbuf", [128, 128], "bfloat16"), "BI": ("sbuf", [128, 128], "bfloat16"), "NBI": ("sbuf", [128, 128], "bfloat16"),
+    "N64": ("sbuf", [128, 128], "bfloat16"), "c64": ("sbuf", [128, 256], "bfloat16"),
+    "pi": ("sbuf", [128, 8], "int32"), "pf": ("sbuf", [128, 8], "float32"),
+    "oh": ("sbuf", [128, 4], "float32"), "jf": ("sbuf", [128, 8], "float32"), "ea": ("sbuf", [128, 12], "float32"),
     "St": ("sbuf", [128, V], "bfloat16"), "Ls": ("sbuf", [128, V], "bfloat16"), "iS0": ("sbuf", [128, V], "bfloat16"),
     "xs": ("sbuf", [128, V], "bfloat16"), "mx": ("sbuf", [128, V], "bfloat16"), "ch": ("sbuf", [128, V], "bfloat16"),
-    "ff": ("sbuf", [128, V], "bfloat16"), "xa": ("sbuf", [128, V], "bfloat16"), "xb": ("sbuf", [128, V], "bfloat16"),
+    "ff": ("sbuf", [128, V + 16], "bfloat16"), "xa": ("sbuf", [128, V], "bfloat16"), "xb": ("sbuf", [128, V], "bfloat16"),
     "dS": ("sbuf", [128, V], "bfloat16"), "acc": ("sbuf", [128, 1024], "float32"),
     "U": ("sbuf", [128, 4], "uint16"), "ido": ("sbuf", [128, 4], "uint16"),
     "id0": ("sbuf", [128, 16], "uint16"), "id1": ("sbuf", [128, 16], "uint16"), "id2": ("sbuf", [128, 16], "uint16"),
@@ -44,14 +51,14 @@ SCRATCH = {
     "Jb": ("sbuf", [128, 192], "bfloat16"), "ki": ("sbuf", [128, 32], "int32"), "ku": ("sbuf", [128, 32], "uint16"),
     "Po": ("sbuf", [128, 128], "float32"), "Pr": ("sbuf", [128, 384], "float32"),
     "Uo": ("sbuf", [128, 192], "uint16"), "Ur": ("sbuf", [128, 576], "uint16"),
-    "sm": ("sbuf", [128, 256], "bfloat16"), "sf": ("sbuf", [128, 192], "float32"),
+    "sm": ("sbuf", [128, 256], "bfloat16"), "Lu": ("sbuf", [128, FW], "float32"),
     "xo": ("sbuf", [128, V], "float32"), "lo": ("sbuf", [128, V], "float32"),
     "pS": ("psum", [128, 512], "float32"), "pX": ("psum", [128, 512], "float32"),
     "pR0": ("psum", [128, 1024], "float32"), "pR1": ("psum", [128, 2048], "float32"),
 }
-PART = {"Sel": ("GC", 0, 2048), "cm": ("GC", 2048, 1024), "junk": ("GC", 3072, 2 * V),
-        "bA": ("GV", 1024, WA), "bB": ("GV", 1024 + WA, WB)}
-POOL = {"v": 44, "s": 30, "t": 16, "g": 10, "y": 12}
+PART = {"Sel": ("GC", 0, 512), "cm": ("GC", 2048, 1024), "junk": ("GC", 3072, 2 * V),
+        "bA": ("GV", 1024, WA), "bB": ("GV", 1024 + WA, WB), "Rg": ("GV", 0, V)}
+POOL = {"v": 44, "s": 32, "t": 16, "g": 8, "y": 22}
 SEMAPHORES = ([q + str(i) for q in POOL for i in range(POOL[q])] + ["ids%d" % t for t in range(3)]
               + ["val%d_%d" % (t, d) for t in range(3) for d in range(3)] + ["li%d" % t for t in range(3)]
               + ["lv%d" % t for t in range(3)] + ["zin", "zout", "zarr", "rep"])
@@ -59,10 +66,10 @@ A = AluOpType
 F = ActivationFunctionType
 
 
-def R(name, lo, hi, step=1):
+def R(name, lo, hi, step=1, rows=(0, 128)):
     if name in PART:
-        return ("R", PART[name][0], PART[name][1] + lo, PART[name][1] + hi, step)
-    return ("R", name, lo, hi, step)
+        return ("R", PART[name][0], PART[name][1] + lo, PART[name][1] + hi, step, rows)
+    return ("R", name, lo, hi, step, rows)
 
 
 def whole(name):
@@ -115,7 +122,7 @@ def main_program(g, core, rank, T, topo):
 
     def ap(a):
         if isinstance(a, tuple) and a[0] == "R":
-            return T[a[1]][:, a[2]:a[3]] if a[4] == 1 else T[a[1]][:, a[2]:a[3]:a[4]]
+            return T[a[1]][a[5][0]:a[5][1], a[2]:a[3]] if a[4] == 1 else T[a[1]][a[5][0]:a[5][1], a[2]:a[3]:a[4]]
         if isinstance(a, tuple) and a[0] == "X":
             return ap(a[1]).indirect(ap(a[2]))
         return a
@@ -173,6 +180,9 @@ def main_program(g, core, rank, T, topo):
     def mm(out, lhsT, rhs, start, stop):
         return call("t", g.tensor.matmul, out, lhsT, rhs, start, stop)
 
+    def summed(out, *terms):
+        together("t", (mm(out, whole(lhsT), rhs, i == 0, i == len(terms) - 1) for i, (lhsT, rhs) in enumerate(terms)))
+
     def iota(out, pattern, base, cm):
         if SCRATCH[out[1]][2] == "int32":
             return call("g", g.iota, out, pattern, base, cm)
@@ -207,55 +217,58 @@ def main_program(g, core, rank, T, topo):
         together("g", (iota(R("W", a, a + n), [[0, n]], 0, 0) for a in zpos[1:]), "zg")
         zpos[1] += n
 
-    lB = load("s", whole("cB"), T.cost[:, 16 * WA:E])
-    load("y", whole("xi"), T.x0[:])
+    def load_costs(b):
+        w, c0 = BW[b], sum(BW[:b])
+        e0 = 16 * (WA + c0)
+        together("y", (load("y", R("cB", c0, c0 + w, 1, (32 * a, 32 * a + 32)), T.cost[:, e0 + 4 * w * a:e0 + 4 * w * (a + 1)])
+                       for a in range(4)))
+
+    load_costs(0)
+    states = load("y", whole("xi"), T.x0[:])
     load("y", whole("d0"), T.drv[:, 0:V])
     load("y", whole("thi"), T.th[:])
+    load_costs(1)
+    load("y", whole("cA"), T.cost[:, 0:16 * WA], after=(states,))
+    load_costs(2)
 
     call("v", g.vector.memset, R("W", 0, ZP), 0.0)
+    iota(whole("kf"), [[0, 16], [1, 16]], 0, 0)
     iota(R("pi", 0, 1), [[0, 1]], 0, 1)
-    iota(whole("kf"), [[0, V // 16], [1, 16]], 0, 0)
+    iota(whole("m16"), [[1, 8], [0, 16]], 0, 0)
     hr, hp = topo.addr(helper)[:2]
     record("g", lambda: g.remote_dma(T.W[:, 0:ZP], T.W[:, 0:ZP], T.sem.zin, T.sem.zout, hp, hr, topo.mask(core, helper)),
            [R("W", 0, ZP)], [], dma=True, fixed=("zout", len(topo.engines(core, helper))))
     arrival("zarr", ZH * len(topo.engines(helper, core)), [R("W", WN - ZH * ZP, WN)])
-    load("y", whole("cA"), T.cost[:, 0:16 * WA], after=(lB,))
-    load("y", whole("fanb"), T.fan[:])
-    iota(whole("m16"), [[1, 8], [0, 16]], 0, 0)
-    iota(whole("mm"), [[1, 128]], 0, 0)
     iota(whole("line"), [[1, V]], CAP + 1 - V, 0)
     iota(whole("Jb"), [[0, 3], [1, 64]], 0, 0)
     iota(whole("ki"), [[1, 16], [256, 2]], 0, 0)
+    iota(whole("mm"), [[1, 128]], 0, 0)
     zero_g(ZG[0])
-    zero_g(ZG[1])
 
-    act(whole("St"), whole("kf"), F.Exp, bias=-64 * LN2, scale=8 * LN2)
-    act(whole("pS"), whole("St"), F.Copy)
-    act(whole("Ls"), whole("St"), F.Copy)
-    act(whole("iS0"), whole("kf"), F.Exp, scale=-8 * LN2)
+    for h in (0, 256):
+        act(R("pS", h, h + 256), whole("kf"), F.Exp, bias=-64 * LN2, scale=8 * LN2)
 
+    zero_v(ZV[0])
     ts(R("pi", 1, 2), R("pi", 0, 1), 15, A.bitwise_and)
     ts(R("pi", 2, 3), R("pi", 0, 1), 4, A.arith_shift_right)
-    zero_v(512)
-    cp(R("pf", 0, 3), R("pi", 0, 3))
-    ts(R("pf", 3, 4), R("pi", 1, 2), 0.5, A.add)
-    zero_v(512)
-    ts(whole("oh"), R("kf", 0, 16), R("pf", 1, 2), A.is_equal)
-    ts(R("jf", 0, 4), R("kf", 0, 4), 16.0, A.mult, R("pf", 3, 4), A.add)
+    ts(R("pi", 3, 4), R("pi", 0, 1), 3, A.bitwise_and)
+    ts(R("pi", 4, 5), R("pi", 0, 1), 2, A.arith_shift_right, 7, A.bitwise_and)
+    zero_v(ZV[1])
+    cp(R("pf", 0, 5), R("pi", 0, 5))
+    ts(R("pf", 5, 6), R("pi", 1, 2), 0.5, A.add)
+    ts(whole("oh"), R("kf", 0, 4), R("pf", 3, 4), A.is_equal)
     ts(whole("Bm"), whole("m16"), R("pf", 2, 3), A.is_equal)
-    ts(whole("B2"), whole("m16"), R("pf", 2, 3), A.is_equal, 2.0, A.mult)
-    ts(whole("NB"), whole("m16"), R("pf", 2, 3), A.is_equal, -1.0, A.mult)
-    for h in (0, 8):
-        together("v", (ts(R("Sel", 128 * i, 128 * i + 128), whole("Bm"), R("oh", i, i + 1), A.mult) for i in range(h, h + 8)))
-    ts(whole("Im"), whole("mm"), R("pf", 0, 1), A.is_equal)
-    ts(whole("N16"), whole("mm"), R("pf", 0, 1), A.is_equal, -float(DEC), A.mult)
+    ts(R("jf", 0, 4), R("kf", 0, 4), 16.0, A.mult, R("pf", 5, 6), A.add)
+    together("v", (ts(R("Sel", 128 * r, 128 * r + 128), whole("m16"), R("pf", 4, 5), A.is_equal, R("oh", r, r + 1), A.mult)
+                   for r in range(4)))
 
-    def convert(name, w):
-        for a in range(0, w, 512):
-            b = min(a + 512, w)
-            tt(R("b" + name, a, b), R("c" + name, a, b), R("pS", 0, b - a), A.mult)
+    def convert(name, a, b):
+        for c in range(a, b, 512):
+            d = min(c + 512, b)
+            tt(R("b" + name, c, d), R("c" + name, c, d), R("pS", 0, d - c), A.mult)
 
-    piece = [16 * WA, 0, 0]
+    runs = [(sum(BW[:b]), BW[b], j) for b in range(len(BW)) for j in range(16)]
+    piece = [16 * WA, 0, 0, 0, 0]
     pending = []
 
     def select(pr, p0, n):
@@ -264,10 +277,14 @@ def main_program(g, core, rank, T, topo):
         c = a
         group[0], group[1] = len(ops), "t"
         while c < b:
-            i, o = divmod(c - 16 * WA, WB)
-            w = min(WB - o, 512 - (c - a) % 512, b - c)
-            mm(R(pr, p0 + c - a, p0 + c - a + w), R("Sel", 128 * i, 128 * i + 128), R("bB", o, o + w), True, True)
-            c += w
+            c0, w, j = runs[piece[3]]
+            o = piece[4]
+            k = min(w - o, 512 - (c - a) % 512, b - c)
+            rows = (32 * (j // 4), 32 * (j // 4) + 32)
+            mm(R(pr, p0 + c - a, p0 + c - a + k), R("Sel", 128 * (j % 4), 128 * (j % 4) + 128, 1, rows),
+               R("bB", c0 + o, c0 + o + k, 1, rows), True, True)
+            c += k
+            piece[3], piece[4] = (piece[3] + 1, 0) if o + k == w else (piece[3], o + k)
         group[0] = group[1] = None
         return R("CT", a, b), R(pr, p0, p0 + b - a)
 
@@ -278,41 +295,30 @@ def main_program(g, core, rank, T, topo):
                 act(*select("pR1", 1024 * (piece[1] % 2), 1024), F.Copy)
 
     def fill_v():
-        if piece[0] < E:
-            piece[2] += 1
-            pending.append(select("pR0", 512 * (piece[2] % 2), 512))
+        pending.append(select("pR0", 0, 1024))
 
     def spread_v():
-        if pending:
-            cp(*pending.pop(0))
-            fill_v()
+        cp(*pending.pop(0))
 
-    def choose(gap=None):
-        scan(whole("ff"), whole("ch"), whole("line"), 0.0, A.add, A.max)
-        for c in (0, 1):
-            ts(R("cm", V * c, V * c + V), whole("ff"), R("jf", c, c + 1), A.is_le, 2.0, A.mult)
-        for c in (2, 3):
-            act(R("junk", V * (c - 2), V * (c - 1)), whole("ff"), F.Sign, bias=R("jf", c, c + 1), scale=-1.0,
-                accum_out=R("acc", 256 * c + 255, 256 * c + 256))
-        for c in (0, 1):
-            scan(R("acc", 256 * c, 256 * c + 256), R("cm", V * c, V * c + 256), R("cm", V * c + 256, V * c + V),
-                 -float(V), A.add, A.add)
-        if gap:
-            gap()
-        ts(whole("U"), R("acc", 255, 1024, 256), 0.5, A.mult, V / 2.0, A.add)
+    def ff(a, b):
+        return R("ff", 16 + a, 16 + b)
+
+    def listed(last, half):
+        ts(whole("ido"), last, 0.5, A.mult, half + V * rank, A.add)
+        ts(whole("U"), last, 0.5, A.mult, half, A.add)
 
     def lists(ids, n, e, p, u, px):
         yield cp(R(e, 0, n), X(whole("fanb"), ids))
         yield cp(R(u, 2 * n, 3 * n), R(e, 0, n))
-        yield ts(R(e, n, 2 * n), R(e, 0, n), 10, A.arith_shift_right)
         yield ts(R(e, 2 * n, 3 * n), R(e, 0, n), 15, A.bitwise_and)
-        yield ts(R("pX", px, px + n), R(e, n, 2 * n), 1.0 / SEG - 1024, A.mult)
+        yield ts(R(e, n, 2 * n), R(e, 0, n), 10, A.arith_shift_right)
         yield tt(R(p, n, 2 * n), R(e, 2 * n, 3 * n), R("pX", 256, 256 + n), A.add)
-        yield tt(R(p, 0, n), R(e, 0, n), R("pX", px, px + n), A.add)
+        yield ts(R("pX", px, px + n), R(e, n, 2 * n), 1.0 / SEG - 1024, A.mult)
         yield ts(R(u, n, 2 * n), R(p, n, 2 * n), float(CAP), A.mult)
+        yield tt(R(p, 0, n), R(e, 0, n), R("pX", px, px + n), A.add)
         yield ts(R(u, 0, n), R(p, 0, n), float(SEG), A.mult, 0.25, A.add)
 
-    def values():
+    def values(t):
         U = whole("U")
         yield cp(R("sm", 0, 64), X(whole("Ls"), U))
         yield tt(R("sm", 64, 128), X(whole("xs"), U), R("sm", 0, 64), A.subtract)
@@ -320,18 +326,23 @@ def main_program(g, core, rank, T, topo):
         yield tt(R("sm", 192, 256), R("sm", 128, 192), R("sm", 0, 64), A.add)
         yield tt(R("VO", 0, 64), X(whole("iS0"), U), R("sm", 192, 256), A.mult)
         yield together("v", (ts(R("VO", 64 * k, 64 * k + 64), R("VO", 0, 64), 2.0 ** (8 * k), A.mult) for k in (1, 2, 3)))
-        yield together("v", (ts(R("VO", 256 * k, 256 * k + 256), R("VO", 0, 256), 2.0 ** (32 * k), A.mult) for k in (1, 2, 3)))
+        for k in (1, 2, 3):
+            if k > KS or not t:
+                ts(R("VO", 256 * k, 256 * k + 256), R("VO", 0, 256), 2.0 ** (32 * k), A.mult)
+            else:
+                act(R("VO", 256 * k, 256 * k + 256), R("VO", 0, 256), F.Copy, scale=2.0 ** (32 * k))
+        yield
 
     def send_ids(t):
-        ts(whole("ido"), R("acc", 255, 1024, 256), 0.5, A.mult, V / 2.0 + V * rank, A.add)
         idt = "id%d" % t
         tr = RemoteDMATransfer(
             dst_ids=[DstId(rid=topo.addr(T.cores[q])[0], pnc=topo.addr(T.cores[q])[1]) for q in peers],
             dma_engine_mask=mask, remote_sem=T.sem["ids%d" % t], srcs=[T.ido[:]],
             dsts=[T[idt][:, 4 * slot[q]:4 * slot[q] + 4] for q in peers])
-        record("g", lambda: g.remote_dma_fused([tr], local_sem=T.sem["li%d" % t]), [whole("ido")], [], dma=True,
-               fixed=("li%d" % t, neng))
+        sent = record("g", lambda: g.remote_dma_fused([tr], local_sem=T.sem["li%d" % t]), [whole("ido")], [], dma=True,
+                      fixed=("li%d" % t, neng))
         arrival("ids%d" % t, 3 * neng, [R(idt, 0, 12)])
+        return sent
 
     def send_values(t):
         vs = "VS%d" % (t % 2)
@@ -350,12 +361,13 @@ def main_program(g, core, rank, T, topo):
         act(R("GV", at, at + 16 * (b - a)), X(win, R(u, n + a, n + b)), F.Identity)
 
     def own_lists(t):
-        a, b = lists(whole("ido"), 64, "Eo", "Po", "Uo", 0), values()
-        for i, who in enumerate("ababababababaaba"):
+        a, b = lists(whole("ido"), 64, "Eo", "Po", "Uo", 0), values(t)
+        for i, who in enumerate(ORDER):
             next(a if who == "a" else b)
             if t and i == 2:
                 cost_gather("Uo", 64, 0, 64, 0)
-        send_values(t)
+            if i == ORDER.rindex("b"):
+                send_values(t)
         cp(X(whole("Ls"), whole("U")), R("sm", 192, 256))
 
     def remote_lists(t):
@@ -364,15 +376,7 @@ def main_program(g, core, rank, T, topo):
 
     def scatter(u, a, b, at):
         w = 16 * (b - a)
-        tt(X(whole("W"), R(u, a, b)), R("GC", at, at + w), R("GV", at, at + w), A.add)
-
-    def ahead(t):
-        if t < RO - 1:
-            together("s", (act(R("dS", k, V, 16), X(R("dr", V * t, V * t + V), R("ku", 2 * k, 2 * k + 2)), F.Identity,
-                               bias=2.0 ** (8 * k - 64), scale=2.0 ** (8 * k - 64)) for k in range(16)))
-        else:
-            tt(whole("xo"), whole("Ls"), whole("pS"), A.mult)
-            act(whole("lo"), whole("xo"), F.Identity, bias=-1.0)
+        return tt(X(whole("W"), R(u, a, b)), R("GC", at, at + w), R("GV", at, at + w), A.add)
 
     def remote_items(t):
         vs = "VS%d" % (t % 2)
@@ -381,138 +385,245 @@ def main_program(g, core, rank, T, topo):
             cost_gather("Ur", 192, a, b, at)
             value_gather(R(vs, 1024 * d, 1024 * d + 1024), "Ur", 192, a, b, at)
             scatter("Ur", a, b, at)
-        if t < RO - 2:
-            ahead(t + 1)
+
+    def scaled_drive(t):
+        together("s", (act(R("dS", k, V, 16), X(R("dr", V * (t - 1), V * t), R("ku", 2 * k, 2 * k + 2)), F.Identity,
+                           bias=2.0 ** (8 * k - 64), scale=2.0 ** (8 * k - 64)) for k in range(16)))
 
     def cells(half, a, b):
         return R("W", half * HALF + SEG * a + SEG - 1, half * HALF + SEG * b, SEG)
 
-    convert("B", WB)
-    spread_s(2)
-    zero_v(Z1)
+    convert("B", 0, BW[0])
+    act(whole("St"), whole("pS"), F.Copy)
+    spread_s(1)
+    zero_v(ZV[2])
     cp(whole("thf"), whole("thi"))
     ts(whole("pX"), whole("xi"), -float(DEC), A.add)
     tt(whole("mx"), whole("pX"), whole("d0"), A.max)
-    spread_s(1)
+    spread_s(2)
     mm(whole("pX"), whole("Bm"), whole("mx"), True, True)
     ts(whole("xa"), whole("mx"), 1.0, A.add)
     tt(whole("xs"), whole("xa"), whole("pS"), A.mult)
     spread_s(1)
     ts(whole("ch"), whole("pX"), whole("thf"), A.is_ge)
-    choose(lambda: convert("A", WA))
+    convert("B", BW[0], BW[0] + BW[1])
+    scan(ff(0, V), whole("ch"), whole("line"), 0.0, A.add, A.max)
+    for c in (0, 1):
+        ts(R("cm", V * c, V * c + V), ff(0, V), R("jf", c, c + 1), A.is_le, 2.0, A.mult)
+    convert("A", 0, WA)
     first = record("y", lambda: g.sync.dma_start(T.CT[0:128:16, 0:16 * WA], ap(whole("bA"))), [whole("bA")], [], dma=True)
-    act(R("pX", 256, 448), whole("Jb"), F.Copy, scale=1.0 / CAP)
-    spread_s(2)
+    load("y", whole("fanb"), T.fan[:])
+    for c in (2, 3):
+        act(R("junk", V * (c - 2), V * (c - 1)), ff(0, V), F.Sign, bias=R("jf", c, c + 1), scale=-1.0,
+            accum_out=R("acc", 256 * c + 255, 256 * c + 256))
+    for c in (0, 1):
+        scan(R("acc", 256 * c, 256 * c + 256), R("cm", V * c, V * c + 256), R("cm", V * c + 256, V * c + V),
+             -float(V), A.add, A.add)
+    spread_s(1)
+    listed(R("acc", 255, 1024, 256), V / 2.0)
     send_ids(0)
+    zero_g(ZG[1])
     zero_g(ZG[2])
-    load("y", R("dr", 0, V), T.drv[:, V:2 * V])
+    convert("B", BW[0] + BW[1], WB)
+    act(R("pX", 256, 448), whole("Jb"), F.Copy, scale=1.0 / CAP)
+    for h in (0, 256):
+        act(R("iS0", h, h + 256), whole("kf"), F.Exp, scale=-8 * LN2)
+    fill_v()
+    spread_s(2)
+    cp(whole("Ls"), whole("St"))
+    ts(R("jf", 4, 5), R("pi", 1, 2), 16.0, A.mult)
+    ts(R("pi", 5, 6), whole("thi"), R("pf", 1, 2), A.add, -1.0, A.add)
+    ts(whole("Im"), whole("mm"), R("pf", 0, 1), A.is_equal)
+    ts(R("pi", 6, 7), R("pi", 5, 6), 4, A.arith_shift_right)
+    ts(whole("ku"), whole("ki"), R("jf", 4, 5), A.add)
+    later = ts(R("pf", 6, 7), R("pi", 6, 7), -1.0, A.mult)
     for r in range(1, 16):
         copied = record("y", (lambda r=r: g.sync.dma_start(T.CT[r:128:16, 0:16 * WA], T.CT[0:128:16, 0:16 * WA])),
-                        [], [], dma=True, fixed=("rep", 16 * 15), after=(first,))
-    load("y", R("dr", V, 3 * V), T.drv[:, 2 * V:RO * V])
-    ts(whole("xa"), whole("mx"), 1.0 - DEC, A.add)
-    ts(R("jf", 4, 5), R("pi", 1, 2), 16.0, A.mult)
-    ts(whole("NI"), whole("mm"), R("pf", 0, 1), A.is_equal, -1.0, A.mult)
-    ts(whole("thS"), whole("St"), whole("thf"), A.mult)
-    ts(whole("ku"), whole("ki"), R("jf", 4, 5), A.add)
-    zero_v(Z2)
-    spread_s(2)
-    own_lists(0)
-    cp(R("GV", 0, 1024), X(whole("VO"), R("Uo", 64, 128)))
-    for n in ZG[3:]:
-        zero_g(n)
-    spread_s(4)
+                        [], [], dma=True, fixed=("rep", 16 * 15), after=(first, later))
+    spread_v()
     zero_v(zend - zpos[0])
-    spread_s(N2)
+    spread_s(NS[0])
     fill_v()
+    spread_s(NS[1])
+    spread_v()
+    own_lists(0)
+    zero_g(ZG[3])
     fill_v()
+    spread_s(NS[2])
+    spread_v()
+    cp(R("GV", 0, 1024), X(whole("VO"), R("Uo", 64, 128)))
     remote_lists(0)
-    ts(whole("xb"), R("dr", 0, V), 1.0, A.add)
-    spread_s(1)
-    while piece[0] < E or pending:
-        spread_v()
-        spread_v()
-        spread_s(1)
+    fill_v()
+    spread_s(len(runs))
+    spread_v()
     record("s", None, [], [], after=(copied,))
-    cost_gather("Uo", 64, 0, 32, 0)
+    cost_gather("Uo", 64, 0, 8, 0)
+    cost_gather("Uo", 64, 8, 32, 128)
     cost_gather("Uo", 64, 32, 64, 512)
-    tt(cells(0, 0, V), whole("xa"), whole("pS"), A.mult)
-    tt(cells(1, 0, V), whole("xb"), whole("pS"), A.mult)
-    scatter("Uo", 0, 32, 0)
+    later = scatter("Uo", 0, 8, 0)
+    load("y", whole("dr"), T.drv[:, V:RO * V], after=(later,))
+    scatter("Uo", 8, 32, 128)
     scatter("Uo", 32, 64, 512)
     remote_items(0)
+    act(whole("N16"), whole("Im"), F.Identity, scale=-float(DEC))
+    scaled_drive(1)
+    summed(R("pR1", 1536, 2048), ("Im", whole("xs")), ("N16", whole("St")))
+    for a, b in ((0, 32), (32, 128), (128, V)):
+        act(cells(0, a, b), R("pR1", 1536 + a, 1536 + b), F.Copy)
+        act(cells(1, a, b), R("dS", a, b), F.Copy)
+    for name, src, k in (("NI", "Im", -1.0), ("TW", "Bm", R("pf", 6, 7)), ("NB", "Bm", -1.0), ("B2", "Bm", 2.0)):
+        act(whole(name), whole(src), F.Identity, scale=k)
 
-    def chunk_tail(c, last):
-        a, b = CH * c, CH * c + CH
-        so = (c % 2) * SOW
-        view = R("SO", so + SEG - 1, so + SOW, SEG)
-        if c == 3:
-            tt(R("mx", a, b), view, R("Ls", a, b), A.max)
-        act(R("xs", a, b), view, F.Copy)
-        if c == 3:
-            sm = R("pR0", 512, 512 + CH)
-            mm(sm, whole("NB"), R("Ls", a, b), True, False)
-            mm(sm, whole("NB"), R("xs", a, b), False, False)
-            mm(sm, whole("B2"), R("mx", a, b), False, True)
-        else:
-            df = R("pR1", 512 * c + CH, 512 * c + 2 * CH)
-            mm(df, whole("NI"), R("Ls", a, b), True, False)
-            mm(df, whole("Im"), R("xs", a, b), False, True)
-            act(R("mx", a, b), df, F.Abs)
-            mm(R("pR0", a, b), whole("Bm"), R("mx", a, b), True, True)
-        if last:
-            tt(R("acc", a, b), view, R("pS", a, b), A.mult)
-            act(R("xo", a, b), R("acc", a, b), F.Identity, bias=-1.0)
+    def view(a, b):
+        return R("SO", SEG * (a % RING) + SEG - 1, SEG * ((b - 1) % RING + 1), SEG)
 
-    def chunk_cells(c):
-        a, b = CH * c, CH * c + CH
-        p0 = 512 * c
-        mm(R("pR1", p0, p0 + CH), whole("Im"), R("xs", a, b), True, False)
-        mm(R("pR1", p0, p0 + CH), whole("N16"), R("St", a, b), False, True)
-        act(cells(0, a, b), R("pR1", p0, p0 + CH), F.Copy)
+    def sums(a, b):
+        return R("pR0", a, b) if a < F0 else R("pR0", 512 + a - F0, 512 + b - F0)
+
+    def take(a, b):
+        act(R("xs", a, b), view(a, b), F.Copy)
+
+    def differ(a, b, between=()):
+        summed(R("pR1", a, b), ("NI", R("Ls", a, b)), ("Im", R("xs", a, b)))
+        for fn, args in between:
+            fn(*args)
+        act(R("mx", a, b), R("pR1", a, b), F.Abs)
+        summed(sums(a, b), ("TW", R("St", a, b)), ("Bm", R("mx", a, b)))
+
+    def mark(a, b):
+        act(R("mx", a, b), sums(a, b), F.Sign)
+        act(R("ch", a, b), R("mx", a, b), F.Relu)
+
+    def count(a, b):
+        scan(ff(a, b), R("ch", a, b), R("line", a, b), ff(a - 1, a) if a else 0.0, A.add, A.max)
+
+    def before(e, a, b, c):
+        act(R("junk", 256 * c, 256 * c + b - a), ff(a, b), F.Sign, bias=R("jf", c, c + 1), scale=-1.0,
+            accum_out=R("ea", 4 * e + c, 4 * e + c + 1))
+
+    def new_cells(a, b):
+        p = R("pR1", 512 + a, 512 + b) if a % 256 == 0 else R("pR1", 1024 + a, 1024 + b)
+        summed(p, ("Im", R("xs", a, b)), ("N16", R("St", a, b)))
+        act(cells(0, a, b), p, F.Copy)
         act(cells(1, a, b), R("dS", a, b), F.Copy)
 
-    for t in range(1, RO):
-        last = t == RO - 1
+    def last_sums():
+        tt(R("mx", F1, V), view(F1, V), R("Ls", F1, V), A.max)
+        take(F1, V)
+        summed(sums(F1, V), ("TW", R("St", F1, V)), ("NB", R("Ls", F1, V)), ("NB", R("xs", F1, V)), ("B2", R("mx", F1, V)))
+
+    def last_marks():
+        ts(R("ch", F0, V), sums(F0, V), 0.0, A.is_gt)
+
+    def choose():
+        h = FW // 2
+        count(F0, V)
         for c in range(4):
-            for k in range(8):
-                a = SEG * (CH * c + 16 * k)
-                so = (c % 2) * SOW + 16 * SEG * k
-                together("v", (scan(R("SO", so, so + 16 * SEG), R("W", a, a + 16 * SEG),
-                                    R("W", HALF + a, HALF + a + 16 * SEG), 0.0, A.max, A.max) for j in (0,)), ("scan", t, c))
-                if k == 0 and c > 0:
-                    chunk_tail(c - 1, last)
-                    if not last:
-                        chunk_cells(c - 1)
-                    if t == RO - 2 and c == 1:
-                        act(whole("xb"), whole("kf"), F.Exp, bias=64 * LN2, scale=-8 * LN2)
-                        act(whole("pS"), whole("xb"), F.Copy)
-        chunk_tail(3, last)
-        tt(R("ch", 0, 3 * CH), R("pR0", 0, 3 * CH), R("thS", 0, 3 * CH), A.is_ge)
-        tt(R("ch", 3 * CH, V), R("pR0", 512, 512 + CH), R("thS", 3 * CH, V), A.is_ge)
-        if last:
-            ox = store("y", T.yx[:], whole("xo"))
+            ts(R("cm", FW * c, FW * c + FW), ff(F0, V), R("jf", c, c + 1), A.is_le, 2.0, A.mult)
+        tt(R("ea", 8, 12), R("ea", 0, 4), R("ea", 4, 8), A.add)
+        together("v", (scan(R("acc", h * c, h * c + h), R("cm", FW * c, FW * c + h), R("cm", FW * c + h, FW * c + FW),
+                            R("ea", 8 + c, 9 + c), A.add, A.add) for c in range(4)))
+        listed(R("acc", h - 1, 4 * h, h), F0 / 2.0)
+
+    def capped(a, b):
+        scan(ff(a, b), R("ch", a, b), R("c64", 0, b - a), ff(a - 1, a), A.add, A.min)
+
+    def gate(a, b):
+        w = b - a
+        summed(R("pR1", 1536, 1536 + w), ("BI", ff(a, b)), ("NBI", ff(a - 1, b - 1)), ("N64", R("c64", 0, w)), ("Im", R("xs", a, b)))
+        summed(R("pR1", 1536 + w, 1536 + 2 * w), ("NBI", ff(a, b)), ("BI", ff(a - 1, b - 1)), ("Im", R("Ls", a, b)))
+
+    def gated(a, b):
+        w = b - a
+        act(R("Rg", 0, 2 * w), R("pR1", 1536, 1536 + 2 * w), F.Relu)
+        summed(R("pR1", 512 + a, 512 + b), ("Im", R("Rg", 0, w)), ("Im", R("Rg", w, 2 * w)), ("NI", R("St", a, b)))
+
+    outs = []
+
+    def out_l(a, b):
+        tt(R("lo", a, b), R("pR1", 512 + a, 512 + b), R("xb", a, b), A.mult)
+        outs.append(store("y", T.yl[:, a:b], R("lo", a, b)))
+
+    def out_x_s(a, b):
+        together("s", (act(R("xo", a + k, b, 16), R("xs", a + k, b, 16), F.Identity, bias=-1.0, scale=2.0 ** (64 - 8 * k))
+                       for k in range(16)))
+        outs.append(store("y", T.yx[:, a:b], R("xo", a, b)))
+
+    def lowered(a, b):
+        summed(R("pR1", 1024 + a, 1024 + b), ("Im", R("xs", a, b)), ("NI", R("St", a, b)))
+
+    def out_x_v(a, b):
+        tt(R("xo", a, b), R("pR1", 1024 + a, 1024 + b), R("xb", a, b), A.mult)
+        outs.append(store("y", T.yx[:, a:b], R("xo", a, b)))
+
+    def last_constants():
+        act(whole("xb"), whole("iS0"), F.Copy, scale=2.0 ** 64)
+        act(whole("pS"), whole("xb"), F.Copy)
+        act(whole("c64"), whole("kf"), F.Identity, bias=float(CAP), scale=0.0)
+        act(ff(-1, 0), R("kf", 0, 1), F.Copy)
+        for name, k in (("BI", BIG), ("NBI", -BIG), ("N64", -BIG / CAP)):
+            act(whole(name), whole("Im"), F.Copy, scale=k)
+
+    def do(*calls):
+        return [(c[0], c[1:]) for c in calls]
+
+    def scans(t, plan):
+        stops = sorted(plan)
+        for a in range(0, V, 16):
+            name = ("scan", t, [n for n in stops if n > a][0])
+            so = SEG * (a % RING)
+            together("v", (scan(R("SO", so, so + 16 * SEG), R("W", SEG * a, SEG * (a + 16)),
+                                R("W", HALF + SEG * a, HALF + SEG * (a + 16)), 0.0, A.max, A.max) for j in (0,)), name)
+            for fn, args in plan.get(a + 16, ()):
+                fn(*args)
+
+    for t in range(1, RO - 1):
+        scaled_drive(t + 1)
+        scans(t, {128: do((take, 0, 128), (new_cells, 0, 128)),
+                  256: do((take, 128, 256), (differ, 0, 256), (mark, 0, 256), (new_cells, 128, 256)),
+                  F0: do((count, 0, 256), (take, 256, F0), (before, 0, 0, 256, 0), (differ, 256, F0), (before, 0, 0, 256, 1),
+                         (mark, 256, F0)),
+                  F1: do((take, F0, F1), (before, 0, 0, 256, 2), (differ, F0, F1), (before, 0, 0, 256, 3)),
+                  V: do((last_sums,), (count, 256, F0), *[(before, 1, 256, F0, c) for c in range(4)])})
+        last_marks()
         choose()
-        if last:
-            U = whole("U")
-            cp(R("sf", 0, 64), X(whole("lo"), U))
-            tt(R("sf", 64, 128), X(whole("xo"), U), R("sf", 0, 64), A.subtract)
-            tt(R("sf", 128, 192), X(whole("ch"), U), R("sf", 64, 128), A.mult)
-            tt(X(whole("lo"), U), R("sf", 128, 192), R("sf", 0, 64), A.add)
-            ol = store("y", T.yl[:], whole("lo"))
-            record("y", None, [], [], after=(ox, ol))
-        else:
-            send_ids(t)
-            chunk_cells(3)
-            own_lists(t)
-            value_gather(whole("VO"), "Uo", 64, 0, OWN1, 0)
-            value_gather(whole("VO"), "Uo", 64, OWN1, 64, 16 * OWN1)
-            if t == RO - 2:
-                ahead(t + 1)
-            scatter("Uo", 0, OWN1, 0)
-            remote_lists(t)
-            scatter("Uo", OWN1, 64, 16 * OWN1)
-            remote_items(t)
+        send_ids(t)
+        new_cells(256, V)
+        own_lists(t)
+        if O1:
+            value_gather(whole("VO"), "Uo", 64, 0, O1, 0)
+        value_gather(whole("VO"), "Uo", 64, O1, 64, 16 * O1)
+        if O1:
+            scatter("Uo", 0, O1, 0)
+        remote_lists(t)
+        scatter("Uo", O1, 64, 16 * O1)
+        remote_items(t)
+        if t == 1:
+            last_constants()
+
+    tt(R("pX", 0, FW), R("Ls", F0, V), R("xb", F0, V), A.mult)
+    act(whole("Lu"), R("pX", 0, FW), F.Identity, bias=-1.0)
+    scans(RO - 1, {128: do((take, 0, 128), (differ, 0, 128), (mark, 0, 128), (out_x_s, 0, 128)),
+                   256: do((capped, 0, 128), (take, 128, 256), (differ, 128, 256, do((gate, 0, 128))), (gated, 0, 128),
+                           (mark, 128, 256)),
+                   F0: do((capped, 128, 256), (take, 256, F0), (differ, 256, F0, do((gate, 128, 256))), (lowered, 128, F0),
+                          (mark, 256, F0), (gated, 128, 256)),
+                   F1: do((take, F0, F1), (differ, F0, F1)),
+                   F1 + 32: do((out_x_v, 128, F0)),
+                   V: do((last_sums,), (capped, 256, F0), (gate, 256, F0), (out_l, 0, 256), (gated, 256, F0))})
+    x1, du = R("acc", 0, FW), R("acc", FW, 2 * FW)
+    tt(x1, view(F0, V), R("pS", F0, V), A.mult)
+    act(R("xo", F0, V), x1, F.Identity, bias=-1.0)
+    outs.append(store("s", T.yx[:, F0:V], R("xo", F0, V)))
+    tt(du, x1, R("pX", 0, FW), A.subtract)
+    last_marks()
+    capped(F0, V)
+    tt(R("pX", FW, 2 * FW), ff(F0, V), ff(F0 - 1, V - 1), A.subtract)
+    tt(R("pX", 2 * FW, 3 * FW), R("pX", FW, 2 * FW), du, A.mult)
+    tt(R("lo", 256, F0), R("pR1", 512 + 256, 512 + F0), R("xb", 256, F0), A.mult)
+    tt(R("lo", F0, V), R("pX", 2 * FW, 3 * FW), whole("Lu"), A.add)
+    outs.append(store("y", T.yl[:, 256:V], R("lo", 256, V)))
+    record("y", None, [], [], after=outs)
 
     known = {q: set() for q in Q}
     snap = {}
@@ -555,17 +666,17 @@ def main_program(g, core, rank, T, topo):
         if o["fn"] is None:
             continue
         ins = o["fn"]()
+        inc = 16 if o["dma"] else 1
         if o["fixed"] is not None:
             if o["fixed"][0] == "rep":
                 ins.then_inc(T.sem.rep, 16)
         elif i in event:
-            ins.then_inc(T.sem[event[i][0]], 1)
+            ins.then_inc(T.sem[event[i][0]], inc)
         elif i in needed:
             n = len(pool[q])
             k = [(turn[q] + j) % n for j in range(n)
                  if pool[q][(turn[q] + j) % n][2] is None or pool[q][(turn[q] + j) % n][2] in snap[i]][0]
             turn[q] = k + 1
-            inc = 16 if o["dma"] else 1
             mine = [i] if o["group"] is None else members[o["group"]]
             pool[q][k][1] += inc * len(mine)
             pool[q][k][2] = mine[-1]

@@ -7,57 +7,74 @@ E = 32768
 SEG = 33
 HALF = SEG * V
 WN = 2 * HALF
-WA = 640
-NS = (3, 3, 4)
-BW = (256, 512, 640)
+WA = 768
+BW = (256, 512, 512)
 WB = sum(BW)
+NS = (4, 3)
+NL = 1
 ZP = 1024
-KS = 1
-O1 = 0
-ORDER = "ababababbabbaaaa"
-ZH = 13
-ZG = (2048, 2048, 2048, 1536)
-ZV = (1536, 1024, 2048, 2048)
-RING = 256
-F0, F1 = 384, 448
+ZH = 12
+ZG = (2048, 2048, 1024, 1280)
+ZV = (1536, 1024, 3072)
+KS = 0
+ORDER = "ababababbaba"
+OWN = (0, 8, 24, 64)
+BETWEEN = (4, 1, 1)
+HS = 1
+CG = 64
+ROUND16 = 1.5 * 2 ** 27
+F0 = 304
+F1 = 432
+CP = 464
+CL = 448
+C0 = 64
+OWN0 = (0, 16, 32, 64)
+BETWEEN0 = (4, 1, 1)
+FA = (0, 1)
+CUTS = (0, 64, 104, 128, 168, 192)
+AHEAD = 64
+CUTS0 = (0, 32, 64, 96, 128, 160, 192)
+AHEAD0 = 48
+GV0 = 1
+GV1 = 0
 FW = V - F0
-BIG = 2.0 ** 70
 LN2 = math.log(2.0)
 
 SCRATCH = {
-    "W": ("sbuf", [128, WN], "bfloat16"), "CT": ("sbuf", [128, E], "bfloat16"),
-    "SO": ("sbuf", [128, RING * SEG], "bfloat16"),
+    "W": ("sbuf", [128, WN], "bfloat16"), "CT": ("sbuf", [128, E], "bfloat16"), "SG": ("sbuf", [128, HALF], "bfloat16"),
     "fanb": ("sbuf", [128, 2048], "int32"), "cA": ("sbuf", [128, WA], "int32"), "cB": ("sbuf", [128, WB], "int32"),
-    "xi": ("sbuf", [128, V], "int32"), "d0": ("sbuf", [128, V], "int32"), "dr": ("sbuf", [128, 3 * V], "int32"),
+    "xi": ("sbuf", [128, V], "int32"), "d0": ("sbuf", [128, V + C0], "int32"), "dr": ("sbuf", [128, 3 * V], "int32"),
     "thi": ("sbuf", [128, 1], "int32"), "thf": ("sbuf", [128, 1], "float32"),
     "VS0": ("sbuf", [128, 3072], "bfloat16"), "VS1": ("sbuf", [128, 3072], "bfloat16"),
     "VO": ("sbuf", [128, 1024], "bfloat16"),
-    "GC": ("sbuf", [128, 4096], "bfloat16"), "GV": ("sbuf", [128, 4096], "bfloat16"),
     "kf": ("sbuf", [128, 256], "bfloat16"), "line": ("sbuf", [128, V], "bfloat16"),
     "m16": ("sbuf", [128, 128], "bfloat16"), "mm": ("sbuf", [128, 128], "bfloat16"),
     "Bm": ("sbuf", [128, 128], "bfloat16"), "B2": ("sbuf", [128, 128], "bfloat16"), "NB": ("sbuf", [128, 128], "bfloat16"),
     "Im": ("sbuf", [128, 128], "bfloat16"), "N16": ("sbuf", [128, 128], "bfloat16"), "NI": ("sbuf", [128, 128], "bfloat16"),
-    "TW": ("sbuf", [128, 128], "bfloat16"), "BI": ("sbuf", [128, 128], "bfloat16"), "NBI": ("sbuf", [128, 128], "bfloat16"),
-    "N64": ("sbuf", [128, 128], "bfloat16"), "c64": ("sbuf", [128, 256], "bfloat16"),
+    "N64": ("sbuf", [128, 128], "bfloat16"), "dd": ("sbuf", [128, V], "bfloat16"),
+    "TW": ("sbuf", [128, 128], "bfloat16"), "c64": ("sbuf", [128, F0], "bfloat16"),
     "pi": ("sbuf", [128, 8], "int32"), "pf": ("sbuf", [128, 8], "float32"),
-    "oh": ("sbuf", [128, 4], "float32"), "jf": ("sbuf", [128, 8], "float32"), "ea": ("sbuf", [128, 12], "float32"),
+    "oh": ("sbuf", [128, 4], "float32"), "jf": ("sbuf", [128, 8], "float32"), "ea": ("sbuf", [128, 8], "float32"),
     "St": ("sbuf", [128, V], "bfloat16"), "Ls": ("sbuf", [128, V], "bfloat16"), "iS0": ("sbuf", [128, V], "bfloat16"),
     "xs": ("sbuf", [128, V], "bfloat16"), "mx": ("sbuf", [128, V], "bfloat16"), "ch": ("sbuf", [128, V], "bfloat16"),
     "ff": ("sbuf", [128, V + 16], "bfloat16"), "xa": ("sbuf", [128, V], "bfloat16"), "xb": ("sbuf", [128, V], "bfloat16"),
+    "jk": ("sbuf", [128, F0], "bfloat16"), "cl": ("sbuf", [128, 4 * FW], "bfloat16"),
     "dS": ("sbuf", [128, V], "bfloat16"), "acc": ("sbuf", [128, 1024], "float32"),
     "U": ("sbuf", [128, 4], "uint16"), "ido": ("sbuf", [128, 4], "uint16"),
     "id0": ("sbuf", [128, 16], "uint16"), "id1": ("sbuf", [128, 16], "uint16"), "id2": ("sbuf", [128, 16], "uint16"),
-    "Eo": ("sbuf", [128, 192], "int32"), "Er": ("sbuf", [128, 576], "int32"),
+    "Eo": ("sbuf", [128, 128], "float32"), "Er": ("sbuf", [128, 384], "float32"),
+    "F64": ("sbuf", [128, 128], "float32"), "G64": ("sbuf", [128, 128], "float32"), "F33": ("sbuf", [128, 128], "float32"),
+    "NH": ("sbuf", [128, 128], "bfloat16"),
     "Jb": ("sbuf", [128, 192], "bfloat16"), "ki": ("sbuf", [128, 32], "int32"), "ku": ("sbuf", [128, 32], "uint16"),
-    "Po": ("sbuf", [128, 128], "float32"), "Pr": ("sbuf", [128, 384], "float32"),
+    "Ho": ("sbuf", [128, 64], "bfloat16"), "Hr": ("sbuf", [128, 192], "bfloat16"),
     "Uo": ("sbuf", [128, 192], "uint16"), "Ur": ("sbuf", [128, 576], "uint16"),
-    "sm": ("sbuf", [128, 256], "bfloat16"), "Lu": ("sbuf", [128, FW], "float32"),
+    "sm": ("sbuf", [128, 256], "bfloat16"),
     "xo": ("sbuf", [128, V], "float32"), "lo": ("sbuf", [128, V], "float32"),
     "pS": ("psum", [128, 512], "float32"), "pX": ("psum", [128, 512], "float32"),
     "pR0": ("psum", [128, 1024], "float32"), "pR1": ("psum", [128, 2048], "float32"),
 }
-PART = {"Sel": ("GC", 0, 512), "cm": ("GC", 2048, 1024), "junk": ("GC", 3072, 2 * V),
-        "bA": ("GV", 1024, WA), "bB": ("GV", 1024 + WA, WB), "Rg": ("GV", 0, V)}
+PART = {"GC": ("SG", 0, 4096), "GV": ("SG", 4096, 4096), "Sel": ("SG", 8192, 512), "cm": ("SG", 8704, 4 * V),
+        "bA": ("SG", 10752, WA), "bB": ("SG", 10752 + WA, WB)}
 POOL = {"v": 44, "s": 32, "t": 16, "g": 8, "y": 22}
 SEMAPHORES = ([q + str(i) for q in POOL for i in range(POOL[q])] + ["ids%d" % t for t in range(3)]
               + ["val%d_%d" % (t, d) for t in range(3) for d in range(3)] + ["li%d" % t for t in range(3)]
@@ -217,19 +234,29 @@ def main_program(g, core, rank, T, topo):
         together("g", (iota(R("W", a, a + n), [[0, n]], 0, 0) for a in zpos[1:]), "zg")
         zpos[1] += n
 
-    def load_costs(b):
+    def load_costs(q, b, quarters=range(4)):
         w, c0 = BW[b], sum(BW[:b])
         e0 = 16 * (WA + c0)
-        together("y", (load("y", R("cB", c0, c0 + w, 1, (32 * a, 32 * a + 32)), T.cost[:, e0 + 4 * w * a:e0 + 4 * w * (a + 1)])
-                       for a in range(4)))
+        together(q, (load(q, R("cB", c0, c0 + w, 1, (32 * a, 32 * a + 32)), T.cost[:, e0 + 4 * w * a:e0 + 4 * w * (a + 1)])
+                     for a in quarters), ("costs", b))
 
-    load_costs(0)
+    load_costs("s", 0, (0, 1))
+    load_costs("y", 0, (2, 3))
     states = load("y", whole("xi"), T.x0[:])
-    load("y", whole("d0"), T.drv[:, 0:V])
+    load("y", whole("d0"), T.drv[:, 0:V + C0])
     load("y", whole("thi"), T.th[:])
-    load_costs(1)
+    load_costs("y", 1)
     load("y", whole("cA"), T.cost[:, 0:16 * WA], after=(states,))
-    load_costs(2)
+    load_costs("y", 2)
+
+    def fan_of(q):
+        return R("fanb", V * q, V * q + V)
+
+    def load_fan(qs):
+        for q in qs:
+            load("y", fan_of(q), T.fan[:, V * q:V * q + V])
+
+    load_fan([rank] + peers[:FA[0]])
 
     call("v", g.vector.memset, R("W", 0, ZP), 0.0)
     iota(whole("kf"), [[0, 16], [1, 16]], 0, 0)
@@ -245,8 +272,12 @@ def main_program(g, core, rank, T, topo):
     iota(whole("mm"), [[1, 128]], 0, 0)
     zero_g(ZG[0])
 
-    for h in (0, 256):
-        act(R("pS", h, h + 256), whole("kf"), F.Exp, bias=-64 * LN2, scale=8 * LN2)
+    def scales(name, h):
+        act(R(name, h, h + 256), whole("kf"), F.Exp, bias=-64 * LN2, scale=8 * LN2)
+
+    scales("pS", 0)
+    scales("Ls", 0)
+    scales("Ls", 256)
 
     zero_v(ZV[0])
     ts(R("pi", 1, 2), R("pi", 0, 1), 15, A.bitwise_and)
@@ -277,14 +308,14 @@ def main_program(g, core, rank, T, topo):
         c = a
         group[0], group[1] = len(ops), "t"
         while c < b:
-            c0, w, j = runs[piece[3]]
-            o = piece[4]
+            c0, w, j = runs[piece[2]]
+            o = piece[3]
             k = min(w - o, 512 - (c - a) % 512, b - c)
             rows = (32 * (j // 4), 32 * (j // 4) + 32)
             mm(R(pr, p0 + c - a, p0 + c - a + k), R("Sel", 128 * (j % 4), 128 * (j % 4) + 128, 1, rows),
                R("bB", c0 + o, c0 + o + k, 1, rows), True, True)
             c += k
-            piece[3], piece[4] = (piece[3] + 1, 0) if o + k == w else (piece[3], o + k)
+            piece[2], piece[3] = (piece[2] + 1, 0) if o + k == w else (piece[2], o + k)
         group[0] = group[1] = None
         return R("CT", a, b), R(pr, p0, p0 + b - a)
 
@@ -303,28 +334,42 @@ def main_program(g, core, rank, T, topo):
     def ff(a, b):
         return R("ff", 16 + a, 16 + b)
 
-    def listed(last, half):
-        ts(whole("ido"), last, 0.5, A.mult, half + V * rank, A.add)
-        ts(whole("U"), last, 0.5, A.mult, half, A.add)
+    def listed(last, k, base):
+        ts(whole("U"), last, k, A.mult, base, A.add)
+        ts(whole("ido"), last, k, A.mult, base + V * rank, A.add)
 
-    def lists(ids, n, e, p, u, px):
-        yield cp(R(e, 0, n), X(whole("fanb"), ids))
-        yield cp(R(u, 2 * n, 3 * n), R(e, 0, n))
-        yield ts(R(e, 2 * n, 3 * n), R(e, 0, n), 15, A.bitwise_and)
-        yield ts(R(e, n, 2 * n), R(e, 0, n), 10, A.arith_shift_right)
-        yield tt(R(p, n, 2 * n), R(e, 2 * n, 3 * n), R("pX", 256, 256 + n), A.add)
-        yield ts(R("pX", px, px + n), R(e, n, 2 * n), 1.0 / SEG - 1024, A.mult)
-        yield ts(R(u, n, 2 * n), R(p, n, 2 * n), float(CAP), A.mult)
-        yield tt(R(p, 0, n), R(e, 0, n), R("pX", px, px + n), A.add)
-        yield ts(R(u, 0, n), R(p, 0, n), float(SEG), A.mult, 0.25, A.add)
+    def lists(ids, n, e, h, u, px, pc):
+        y, y16, hi = R(e, 0, n), R(e, n, 2 * n), R(h, 0, n)
+        place, cell = R("pX", px, px + n), R(pc, 256 + px, 256 + px + n)
+        if n == CAP:
+            yield cp(R(u, 2 * n, 3 * n), X(fan_of(rank), ids))
+            yield ts(y, X(fan_of(rank), ids), -7.5, A.add)
+        else:
+            yield ts(y, X(whole("fanb"), ids), -7.5, A.add)
+            yield ts(R(u, 2 * n, 3 * n), y, 7.75, A.add)
+        ts(y16, y, ROUND16, A.add, ROUND16, A.subtract)
+        yield summed(place, ("Im", R("Jb", 0, n)), ("F64", y), ("G64", y16))
+        if n == CAP or not HS:
+            ts(hi, y, 1.0 / 1024, A.mult, 159.5078, A.add)
+        else:
+            act(hi, y, F.Identity, scale=1.0 / 1024, bias=159.5078)
+        yield summed(cell, ("F33", y), ("NH", hi), ("Im", hi))
+        yield ts(R(u, n, 2 * n), place, 7.5 * CAP + 0.25, A.add)
+        yield ts(R(u, 0, n), cell, 7.5 * SEG + 160.0 * (1024 * SEG - 1), A.add, 0.25, A.add)
 
     def values(t):
         U = whole("U")
-        yield cp(R("sm", 0, 64), X(whole("Ls"), U))
-        yield tt(R("sm", 64, 128), X(whole("xs"), U), R("sm", 0, 64), A.subtract)
-        yield tt(R("sm", 128, 192), X(whole("ch"), U), R("sm", 64, 128), A.mult)
-        yield tt(R("sm", 192, 256), R("sm", 128, 192), R("sm", 0, 64), A.add)
-        yield tt(R("VO", 0, 64), X(whole("iS0"), U), R("sm", 192, 256), A.mult)
+        if t:
+            yield cp(R("sm", 0, 64), X(whole("ch"), U))
+            yield tt(R("sm", 64, 128), X(whole("dd"), U), R("sm", 0, 64), A.mult)
+            yield tt(R("sm", 192, 256), X(whole("Ls"), U), R("sm", 64, 128), A.add)
+            yield tt(R("VO", 0, 64), X(whole("iS0"), U), R("sm", 192, 256), A.mult)
+        else:
+            yield cp(R("sm", 0, 64), X(whole("mx"), U))
+            yield tt(R("sm", 64, 128), X(whole("ch"), U), R("sm", 0, 64), A.mult)
+            yield ts(R("sm", 128, 192), R("sm", 64, 128), 1.0, A.add)
+            yield ts(R("VO", 0, 64), R("sm", 64, 128), 1.0, A.add, 2.0 ** -64, A.mult)
+            yield tt(R("sm", 192, 256), X(whole("Ls"), U), R("sm", 128, 192), A.mult)
         yield together("v", (ts(R("VO", 64 * k, 64 * k + 64), R("VO", 0, 64), 2.0 ** (8 * k), A.mult) for k in (1, 2, 3)))
         for k in (1, 2, 3):
             if k > KS or not t:
@@ -339,10 +384,9 @@ def main_program(g, core, rank, T, topo):
             dst_ids=[DstId(rid=topo.addr(T.cores[q])[0], pnc=topo.addr(T.cores[q])[1]) for q in peers],
             dma_engine_mask=mask, remote_sem=T.sem["ids%d" % t], srcs=[T.ido[:]],
             dsts=[T[idt][:, 4 * slot[q]:4 * slot[q] + 4] for q in peers])
-        sent = record("g", lambda: g.remote_dma_fused([tr], local_sem=T.sem["li%d" % t]), [whole("ido")], [], dma=True,
-                      fixed=("li%d" % t, neng))
+        record("g", lambda: g.remote_dma_fused([tr], local_sem=T.sem["li%d" % t]), [whole("ido")], [], dma=True,
+               fixed=("li%d" % t, neng))
         arrival("ids%d" % t, 3 * neng, [R(idt, 0, 12)])
-        return sent
 
     def send_values(t):
         vs = "VS%d" % (t % 2)
@@ -361,28 +405,41 @@ def main_program(g, core, rank, T, topo):
         act(R("GV", at, at + 16 * (b - a)), X(win, R(u, n + a, n + b)), F.Identity)
 
     def own_lists(t):
-        a, b = lists(whole("ido"), 64, "Eo", "Po", "Uo", 0), values(t)
+        a, b = lists(whole("U"), 64, "Eo", "Ho", "Uo", 0, "pS"), values(t)
         for i, who in enumerate(ORDER):
             next(a if who == "a" else b)
-            if t and i == 2:
-                cost_gather("Uo", 64, 0, 64, 0)
+            if i == 0:
+                cost_gather("Uo", 64, 0, CG, 0)
             if i == ORDER.rindex("b"):
                 send_values(t)
         cp(X(whole("Ls"), whole("U")), R("sm", 192, 256))
-
-    def remote_lists(t):
-        for c in lists(R("id%d" % t, 0, 12), 192, "Er", "Pr", "Ur", 64):
-            pass
 
     def scatter(u, a, b, at):
         w = 16 * (b - a)
         return tt(X(whole("W"), R(u, a, b)), R("GC", at, at + w), R("GV", at, at + w), A.add)
 
-    def remote_items(t):
+    def items(t):
+        own, between = (OWN, BETWEEN) if t else (OWN0, BETWEEN0)
+        for a, b in zip(own, own[1:]):
+            if not t:
+                cost_gather("Uo", 64, a, b, 16 * a)
+            if t or a >= own[GV0]:
+                value_gather(whole("VO"), "Uo", 64, a, b, 16 * a)
+            if t and CG < 64 and b == OWN[2]:
+                cost_gather("Uo", 64, CG, 64, 16 * CG)
+        theirs = lists(R("id%d" % t, 0, 12), 192, "Er", "Hr", "Ur", 64, "pS")
+        for (a, b), n in zip(zip(own, own[1:]), between):
+            scatter("Uo", a, b, 16 * a)
+            for i in range(n):
+                next(theirs)
         vs = "VS%d" % (t % 2)
-        for a, b in ((0, 64), (64, 128), (128, 160), (160, 192)):
+        done = 0
+        cuts, ahead = (CUTS, AHEAD) if t else (CUTS0, AHEAD0)
+        for a, b in zip(cuts, cuts[1:]):
             at, d = 1024 + 16 * a, a // 64
-            cost_gather("Ur", 192, a, b, at)
+            if done < b:
+                cost_gather("Ur", 192, done, max(b, ahead), 1024 + 16 * done)
+                done = max(b, ahead)
             value_gather(R(vs, 1024 * d, 1024 * d + 1024), "Ur", 192, a, b, at)
             scatter("Ur", a, b, at)
 
@@ -393,101 +450,101 @@ def main_program(g, core, rank, T, topo):
     def cells(half, a, b):
         return R("W", half * HALF + SEG * a + SEG - 1, half * HALF + SEG * b, SEG)
 
+    def bank(k, a, b):
+        return R("pR1", 512 * k + a, 512 * k + b)
+
     convert("B", 0, BW[0])
-    act(whole("St"), whole("pS"), F.Copy)
+    scales("pS", 256)
     spread_s(1)
     zero_v(ZV[2])
-    cp(whole("thf"), whole("thi"))
     ts(whole("pX"), whole("xi"), -float(DEC), A.add)
-    tt(whole("mx"), whole("pX"), whole("d0"), A.max)
+    cp(whole("thf"), whole("thi"))
+    ts(R("pi", 5, 6), whole("thi"), R("pf", 1, 2), A.add, -1.0, A.add)
+    tt(whole("mx"), whole("pX"), R("d0", 0, V), A.max)
     spread_s(2)
     mm(whole("pX"), whole("Bm"), whole("mx"), True, True)
-    ts(whole("xa"), whole("mx"), 1.0, A.add)
-    tt(whole("xs"), whole("xa"), whole("pS"), A.mult)
+    convert("B", BW[0], BW[0] + BW[1])
     spread_s(1)
     ts(whole("ch"), whole("pX"), whole("thf"), A.is_ge)
-    convert("B", BW[0], BW[0] + BW[1])
+    ts(whole("xa"), whole("mx"), 1.0 - DEC, A.add)
     scan(ff(0, V), whole("ch"), whole("line"), 0.0, A.add, A.max)
-    for c in (0, 1):
+    ts(R("jf", 4, 5), R("pi", 1, 2), 16.0, A.mult)
+    ts(whole("Im"), whole("mm"), R("pf", 0, 1), A.is_equal)
+    for c in range(4):
         ts(R("cm", V * c, V * c + V), ff(0, V), R("jf", c, c + 1), A.is_le, 2.0, A.mult)
     convert("A", 0, WA)
     first = record("y", lambda: g.sync.dma_start(T.CT[0:128:16, 0:16 * WA], ap(whole("bA"))), [whole("bA")], [], dma=True)
-    load("y", whole("fanb"), T.fan[:])
-    for c in (2, 3):
-        act(R("junk", V * (c - 2), V * (c - 1)), ff(0, V), F.Sign, bias=R("jf", c, c + 1), scale=-1.0,
-            accum_out=R("acc", 256 * c + 255, 256 * c + 256))
-    for c in (0, 1):
-        scan(R("acc", 256 * c, 256 * c + 256), R("cm", V * c, V * c + 256), R("cm", V * c + 256, V * c + V),
-             -float(V), A.add, A.add)
-    spread_s(1)
-    listed(R("acc", 255, 1024, 256), V / 2.0)
-    send_ids(0)
-    zero_g(ZG[1])
-    zero_g(ZG[2])
-    convert("B", BW[0] + BW[1], WB)
-    act(R("pX", 256, 448), whole("Jb"), F.Copy, scale=1.0 / CAP)
-    for h in (0, 256):
-        act(R("iS0", h, h + 256), whole("kf"), F.Exp, scale=-8 * LN2)
-    fill_v()
-    spread_s(2)
-    cp(whole("Ls"), whole("St"))
-    ts(R("jf", 4, 5), R("pi", 1, 2), 16.0, A.mult)
-    ts(R("pi", 5, 6), whole("thi"), R("pf", 1, 2), A.add, -1.0, A.add)
-    ts(whole("Im"), whole("mm"), R("pf", 0, 1), A.is_equal)
+    load_fan(peers[FA[0]:FA[1]])
+    together("v", (scan(R("GC", 128 * c, 128 * c + 128), R("cm", 256 * c, 256 * c + 128), R("cm", 256 * c + 128, 256 * c + 256),
+                        0.0, A.add, A.add) for c in range(8)))
     ts(R("pi", 6, 7), R("pi", 5, 6), 4, A.arith_shift_right)
     ts(whole("ku"), whole("ki"), R("jf", 4, 5), A.add)
-    later = ts(R("pf", 6, 7), R("pi", 6, 7), -1.0, A.mult)
-    for r in range(1, 16):
-        copied = record("y", (lambda r=r: g.sync.dma_start(T.CT[r:128:16, 0:16 * WA], T.CT[0:128:16, 0:16 * WA])),
-                        [], [], dma=True, fixed=("rep", 16 * 15), after=(first, later))
-    spread_v()
-    zero_v(zend - zpos[0])
-    spread_s(NS[0])
+    tt(R("ea", 4, 8), R("GC", 127, 1024, 256), R("GC", 255, 1024, 256), A.add)
+    ts(R("pf", 6, 7), R("pi", 6, 7), -1.0, A.mult)
+    spread_s(2)
+    listed(R("ea", 4, 8), 0.5, 0.0)
+    send_ids(0)
+    zero_g(ZG[1])
+    convert("B", BW[0] + BW[1], WB)
     fill_v()
-    spread_s(NS[1])
-    spread_v()
-    own_lists(0)
+    spread_s(2)
+    scaled = {0: ("F64", float(CAP)), 1: ("G64", -float(CAP)), 3: ("F33", float(SEG)), 5: ("NH", -1024.0 * SEG)}
+    for i, c in enumerate(values(0)):
+        if i in scaled:
+            later = ts(whole(scaled[i][0]), whole("mm"), R("pf", 0, 1), A.is_equal, scaled[i][1], A.mult)
+        if i == 1:
+            for r in range(1, 16):
+                copied = record("y", (lambda r=r: g.sync.dma_start(T.CT[r:128:16, 0:16 * WA], T.CT[0:128:16, 0:16 * WA])),
+                                [], [], dma=True, fixed=("rep", 16 * 15), after=(first, later))
+            load_fan(peers[FA[1]:])
+    record("g", None, [], [], after=(first,))
+    zero_g(ZG[2])
+    send_values(0)
+    cp(X(whole("Ls"), whole("U")), R("sm", 192, 256))
     zero_g(ZG[3])
-    fill_v()
-    spread_s(NS[2])
+    rest = zend - zpos[0]
     spread_v()
-    cp(R("GV", 0, 1024), X(whole("VO"), R("Uo", 64, 128)))
-    remote_lists(0)
-    fill_v()
+    mine = lists(whole("U"), 64, "Eo", "Ho", "Uo", 0, "pX")
+    for i, n in enumerate(NS):
+        spread_s(n)
+        fill_v()
+        if i == len(NS) - 1:
+            spread_s(NL)
+            for j in range(4):
+                next(mine)
+        zero_v(rest // len(NS) // 16 * 16 if i < len(NS) - 1 else zend - zpos[0])
+        spread_v()
     spread_s(len(runs))
-    spread_v()
+    for c in mine:
+        pass
+    ts(R("xb", 0, C0), R("d0", V, V + C0), 1.0, A.add)
+    cp(R("GV", 0, 16 * OWN0[GV0]), X(whole("VO"), R("Uo", 64, 64 + OWN0[GV0])))
     record("s", None, [], [], after=(copied,))
-    cost_gather("Uo", 64, 0, 8, 0)
-    cost_gather("Uo", 64, 8, 32, 128)
-    cost_gather("Uo", 64, 32, 64, 512)
-    later = scatter("Uo", 0, 8, 0)
-    load("y", whole("dr"), T.drv[:, V:RO * V], after=(later,))
-    scatter("Uo", 8, 32, 128)
-    scatter("Uo", 32, 64, 512)
-    remote_items(0)
-    act(whole("N16"), whole("Im"), F.Identity, scale=-float(DEC))
+    tt(cells(1, 0, C0), R("xb", 0, C0), R("pS", 0, C0), A.mult)
+    later = tt(cells(0, 0, V), whole("xa"), whole("pS"), A.mult)
+    load("y", R("dr", 0, V), T.drv[:, V:2 * V], after=(later,))
+    items(0)
+    load("y", R("dr", V, 3 * V), T.drv[:, 2 * V:RO * V], after=(len(ops) - 7,))
     scaled_drive(1)
-    summed(R("pR1", 1536, 2048), ("Im", whole("xs")), ("N16", whole("St")))
-    for a, b in ((0, 32), (32, 128), (128, V)):
-        act(cells(0, a, b), R("pR1", 1536 + a, 1536 + b), F.Copy)
-        act(cells(1, a, b), R("dS", a, b), F.Copy)
-    for name, src, k in (("NI", "Im", -1.0), ("TW", "Bm", R("pf", 6, 7)), ("NB", "Bm", -1.0), ("B2", "Bm", 2.0)):
+    act(cells(1, C0, V), R("dS", C0, V), F.Copy)
+    for name, src, k in (("NI", "Im", -1.0), ("TW", "Bm", R("pf", 6, 7)), ("NB", "Bm", -1.0), ("B2", "Bm", 2.0),
+                         ("N16", "Im", -float(DEC))):
         act(whole(name), whole(src), F.Identity, scale=k)
+    for h in (0, 256):
+        scales("St", h)
+        act(R("iS0", h, h + 256), whole("kf"), F.Exp, scale=-8 * LN2)
 
     def view(a, b):
-        return R("SO", SEG * (a % RING) + SEG - 1, SEG * ((b - 1) % RING + 1), SEG)
+        return R("SG", SEG * a + SEG - 1, SEG * b, SEG)
 
     def sums(a, b):
-        return R("pR0", a, b) if a < F0 else R("pR0", 512 + a - F0, 512 + b - F0)
+        return R("pR0", a, b) if a < F0 else R("pR0", 512 + a, 512 + b) if a < F1 else R("pS", a - F1, b - F1)
 
-    def take(a, b):
-        act(R("xs", a, b), view(a, b), F.Copy)
+    def differ(a, b):
+        summed(bank(0, a, b), ("NI", R("Ls", a, b)), ("Im", view(a, b)))
 
-    def differ(a, b, between=()):
-        summed(R("pR1", a, b), ("NI", R("Ls", a, b)), ("Im", R("xs", a, b)))
-        for fn, args in between:
-            fn(*args)
-        act(R("mx", a, b), R("pR1", a, b), F.Abs)
+    def summed_abs(a, b):
+        act(R("mx", a, b), bank(0, a, b), F.Abs)
         summed(sums(a, b), ("TW", R("St", a, b)), ("Bm", R("mx", a, b)))
 
     def mark(a, b):
@@ -497,72 +554,70 @@ def main_program(g, core, rank, T, topo):
     def count(a, b):
         scan(ff(a, b), R("ch", a, b), R("line", a, b), ff(a - 1, a) if a else 0.0, A.add, A.max)
 
-    def before(e, a, b, c):
-        act(R("junk", 256 * c, 256 * c + b - a), ff(a, b), F.Sign, bias=R("jf", c, c + 1), scale=-1.0,
-            accum_out=R("ea", 4 * e + c, 4 * e + c + 1))
+    def before(c):
+        act(R(("xa", "jk")[c % 2], 0, F0), ff(0, F0), F.Sign, bias=R("jf", c, c + 1), scale=-1.0, accum_out=R("ea", c, c + 1))
 
-    def new_cells(a, b):
-        p = R("pR1", 512 + a, 512 + b) if a % 256 == 0 else R("pR1", 1024 + a, 1024 + b)
-        summed(p, ("Im", R("xs", a, b)), ("N16", R("St", a, b)))
-        act(cells(0, a, b), p, F.Copy)
+    def fallen(k, a, b):
+        summed(bank(k, a, b), ("Im", view(a, b)), ("N16", R("St", a, b)))
+
+    def fall_cells(k, a, b):
+        act(cells(0, a, b), bank(k, a, b), F.Copy)
+
+    def drive_cells(a, b):
         act(cells(1, a, b), R("dS", a, b), F.Copy)
 
     def last_sums():
-        tt(R("mx", F1, V), view(F1, V), R("Ls", F1, V), A.max)
-        take(F1, V)
-        summed(sums(F1, V), ("TW", R("St", F1, V)), ("NB", R("Ls", F1, V)), ("NB", R("xs", F1, V)), ("B2", R("mx", F1, V)))
+        for a, b in ((F1, V - 16), (V - 16, V)):
+            tt(R("mx", a, b), view(a, b), R("Ls", a, b), A.max)
+        summed(sums(F1, V), ("TW", R("St", F1, V)), ("NB", R("Ls", F1, V)), ("NB", view(F1, V)), ("B2", R("mx", F1, V)))
 
-    def last_marks():
-        ts(R("ch", F0, V), sums(F0, V), 0.0, A.is_gt)
+    def last_marks(run):
+        ts(R("ch", F0, F1), sums(F0, F1), 0.0, A.is_gt)
+        run(F0, F1)
+        ts(R("ch", F1, V), sums(F1, V), 0.0, A.is_gt)
+        run(F1, V)
 
     def choose():
         h = FW // 2
-        count(F0, V)
         for c in range(4):
-            ts(R("cm", FW * c, FW * c + FW), ff(F0, V), R("jf", c, c + 1), A.is_le, 2.0, A.mult)
-        tt(R("ea", 8, 12), R("ea", 0, 4), R("ea", 4, 8), A.add)
-        together("v", (scan(R("acc", h * c, h * c + h), R("cm", FW * c, FW * c + h), R("cm", FW * c + h, FW * c + FW),
-                            R("ea", 8 + c, 9 + c), A.add, A.add) for c in range(4)))
-        listed(R("acc", h - 1, 4 * h, h), F0 / 2.0)
+            if c == 3:
+                ts(R("ea", 4, 8), R("ea", 0, 4), 0.5, A.mult, F0 / 2.0 - 256, A.add)
+            ts(R("cl", FW * c, FW * c + FW), ff(F0, V), R("jf", c, c + 1), A.is_le)
+        together("v", (scan(R("xs", h * c, h * c + h), R("cl", FW * c, FW * c + h), R("cl", FW * c + h, FW * c + FW),
+                            R("ea", 4 + c, 5 + c), A.add, A.add) for c in range(4)))
+        listed(R("xs", h - 1, 4 * h, h), 1.0, 256.0)
+
+    outs = []
+
+    def kept(a, b):
+        act(R("dd", a, b), bank(0, a, b), F.Copy)
 
     def capped(a, b):
         scan(ff(a, b), R("ch", a, b), R("c64", 0, b - a), ff(a - 1, a), A.add, A.min)
 
-    def gate(a, b):
-        w = b - a
-        summed(R("pR1", 1536, 1536 + w), ("BI", ff(a, b)), ("NBI", ff(a - 1, b - 1)), ("N64", R("c64", 0, w)), ("Im", R("xs", a, b)))
-        summed(R("pR1", 1536 + w, 1536 + 2 * w), ("NBI", ff(a, b)), ("BI", ff(a - 1, b - 1)), ("Im", R("Ls", a, b)))
+    def stepped(a, b):
+        summed(bank(3, a, b), ("Im", ff(a, b)), ("NI", ff(a - 1, b - 1)))
 
     def gated(a, b):
-        w = b - a
-        act(R("Rg", 0, 2 * w), R("pR1", 1536, 1536 + 2 * w), F.Relu)
-        summed(R("pR1", 512 + a, 512 + b), ("Im", R("Rg", 0, w)), ("Im", R("Rg", w, 2 * w)), ("NI", R("St", a, b)))
-
-    outs = []
+        tt(R("mx", a, b), bank(3, a, b), R("dd", a, b), A.mult)
+        summed(bank(1, a, b), ("Im", R("Ls", a, b)), ("NI", R("St", a, b)), ("Im", R("mx", a, b)))
 
     def out_l(a, b):
-        tt(R("lo", a, b), R("pR1", 512 + a, 512 + b), R("xb", a, b), A.mult)
+        tt(R("lo", a, b), bank(1, a, b), R("xb", a, b), A.mult)
         outs.append(store("y", T.yl[:, a:b], R("lo", a, b)))
 
-    def out_x_s(a, b):
-        together("s", (act(R("xo", a + k, b, 16), R("xs", a + k, b, 16), F.Identity, bias=-1.0, scale=2.0 ** (64 - 8 * k))
-                       for k in range(16)))
-        outs.append(store("y", T.yx[:, a:b], R("xo", a, b)))
-
     def lowered(a, b):
-        summed(R("pR1", 1024 + a, 1024 + b), ("Im", R("xs", a, b)), ("NI", R("St", a, b)))
+        summed(bank(2, a, b), ("Im", view(a, b)), ("NI", R("St", a, b)))
 
-    def out_x_v(a, b):
-        tt(R("xo", a, b), R("pR1", 1024 + a, 1024 + b), R("xb", a, b), A.mult)
-        outs.append(store("y", T.yx[:, a:b], R("xo", a, b)))
+    def out_x(a, b):
+        tt(R("xo", a, b), bank(2, a, b), R("xb", a, b), A.mult)
+        outs.append(store("s", T.yx[:, a:b], R("xo", a, b)))
 
     def last_constants():
         act(whole("xb"), whole("iS0"), F.Copy, scale=2.0 ** 64)
-        act(whole("pS"), whole("xb"), F.Copy)
-        act(whole("c64"), whole("kf"), F.Identity, bias=float(CAP), scale=0.0)
+        act(whole("c64"), R("line", 0, F0), F.Identity, bias=float(CAP), scale=0.0)
         act(ff(-1, 0), R("kf", 0, 1), F.Copy)
-        for name, k in (("BI", BIG), ("NBI", -BIG), ("N64", -BIG / CAP)):
-            act(whole(name), whole("Im"), F.Copy, scale=k)
+        act(whole("N64"), whole("Im"), F.Copy, scale=-1.0 / CAP)
 
     def do(*calls):
         return [(c[0], c[1:]) for c in calls]
@@ -571,58 +626,44 @@ def main_program(g, core, rank, T, topo):
         stops = sorted(plan)
         for a in range(0, V, 16):
             name = ("scan", t, [n for n in stops if n > a][0])
-            so = SEG * (a % RING)
-            together("v", (scan(R("SO", so, so + 16 * SEG), R("W", SEG * a, SEG * (a + 16)),
+            together("v", (scan(R("SG", SEG * a, SEG * (a + 16)), R("W", SEG * a, SEG * (a + 16)),
                                 R("W", HALF + SEG * a, HALF + SEG * (a + 16)), 0.0, A.max, A.max) for j in (0,)), name)
             for fn, args in plan.get(a + 16, ()):
                 fn(*args)
 
     for t in range(1, RO - 1):
         scaled_drive(t + 1)
-        scans(t, {128: do((take, 0, 128), (new_cells, 0, 128)),
-                  256: do((take, 128, 256), (differ, 0, 256), (mark, 0, 256), (new_cells, 128, 256)),
-                  F0: do((count, 0, 256), (take, 256, F0), (before, 0, 0, 256, 0), (differ, 256, F0), (before, 0, 0, 256, 1),
-                         (mark, 256, F0)),
-                  F1: do((take, F0, F1), (before, 0, 0, 256, 2), (differ, F0, F1), (before, 0, 0, 256, 3)),
-                  V: do((last_sums,), (count, 256, F0), *[(before, 1, 256, F0, c) for c in range(4)])})
-        last_marks()
+        if t == RO - 2:
+            last_constants()
+        plan = {F0: do((differ, 0, F0), (fallen, 1, 0, F0), (drive_cells, 0, F0), (summed_abs, 0, F0), (fall_cells, 1, 0, F0),
+                       (mark, 0, F0), (kept, 0, F0)),
+                F1: do((differ, F0, F1), (summed_abs, F0, F1)),
+                V - 16: [], V: do((last_sums,), (differ, F1, V), (fallen, 2, F0, V))}
+        plan[CP] = plan.get(CP, []) + do((count, 0, F0), *[(before, c) for c in range(4)])
+        scans(t, plan)
+        last_marks(count)
         choose()
         send_ids(t)
-        new_cells(256, V)
+        kept(F0, V)
+        fall_cells(2, F0, V)
+        drive_cells(F0, V)
         own_lists(t)
-        if O1:
-            value_gather(whole("VO"), "Uo", 64, 0, O1, 0)
-        value_gather(whole("VO"), "Uo", 64, O1, 64, 16 * O1)
-        if O1:
-            scatter("Uo", 0, O1, 0)
-        remote_lists(t)
-        scatter("Uo", O1, 64, 16 * O1)
-        remote_items(t)
-        if t == 1:
-            last_constants()
+        items(t)
 
-    tt(R("pX", 0, FW), R("Ls", F0, V), R("xb", F0, V), A.mult)
-    act(whole("Lu"), R("pX", 0, FW), F.Identity, bias=-1.0)
-    scans(RO - 1, {128: do((take, 0, 128), (differ, 0, 128), (mark, 0, 128), (out_x_s, 0, 128)),
-                   256: do((capped, 0, 128), (take, 128, 256), (differ, 128, 256, do((gate, 0, 128))), (gated, 0, 128),
-                           (mark, 128, 256)),
-                   F0: do((capped, 128, 256), (take, 256, F0), (differ, 256, F0, do((gate, 128, 256))), (lowered, 128, F0),
-                          (mark, 256, F0), (gated, 128, 256)),
-                   F1: do((take, F0, F1), (differ, F0, F1)),
-                   F1 + 32: do((out_x_v, 128, F0)),
-                   V: do((last_sums,), (capped, 256, F0), (gate, 256, F0), (out_l, 0, 256), (gated, 256, F0))})
-    x1, du = R("acc", 0, FW), R("acc", FW, 2 * FW)
-    tt(x1, view(F0, V), R("pS", F0, V), A.mult)
-    act(R("xo", F0, V), x1, F.Identity, bias=-1.0)
-    outs.append(store("s", T.yx[:, F0:V], R("xo", F0, V)))
-    tt(du, x1, R("pX", 0, FW), A.subtract)
-    last_marks()
-    capped(F0, V)
-    tt(R("pX", FW, 2 * FW), ff(F0, V), ff(F0 - 1, V - 1), A.subtract)
-    tt(R("pX", 2 * FW, 3 * FW), R("pX", FW, 2 * FW), du, A.mult)
-    tt(R("lo", 256, F0), R("pR1", 512 + 256, 512 + F0), R("xb", 256, F0), A.mult)
-    tt(R("lo", F0, V), R("pX", 2 * FW, 3 * FW), whole("Lu"), A.add)
-    outs.append(store("y", T.yl[:, 256:V], R("lo", 256, V)))
+    plan = {F0: do((differ, 0, F0), (lowered, 0, F0), (summed_abs, 0, F0), (kept, 0, F0), (mark, 0, F0)),
+            F0 + 48: do((out_x, 0, F0)),
+            F1: do((differ, F0, F1), (summed_abs, F0, F1)),
+            V - 16: do((gated, 0, F0)),
+            V: do((last_sums,), (differ, F1, V), (lowered, F0, V), (out_l, 0, F0))}
+    plan[CL] = plan.get(CL, []) + do((capped, 0, F0), (stepped, 0, F0))
+    scans(RO - 1, plan)
+    last_marks(capped)
+    summed(bank(3, F0, V), ("N64", R("c64", 0, FW)), ("Im", ff(F0, V)), ("NI", ff(F0 - 1, V - 1)))
+    out_x(F0, V)
+    tt(R("acc", 0, FW), bank(0, F0, V), R("xb", F0, V), A.mult)
+    tt(R("pX", 0, FW), bank(3, F0, V), R("acc", 0, FW), A.mult)
+    tt(R("lo", F0, V), R("pX", 0, FW), R("xo", F0, V), A.add)
+    outs.append(store("y", T.yl[:, F0:V], R("lo", F0, V)))
     record("y", None, [], [], after=outs)
 
     known = {q: set() for q in Q}
@@ -641,6 +682,8 @@ def main_program(g, core, rank, T, topo):
             if d not in known[q]:
                 waits.append(d)
                 known[q] |= snap[d] | {d}
+                if not ops[d]["dma"]:
+                    known[q] |= {j for j in range(d) if ops[j]["q"] == ops[d]["q"] and not ops[j]["dma"]}
                 if ops[d]["fixed"] is not None:
                     known[q] |= {j for j in range(i) if ops[j]["fixed"] == ops[d]["fixed"]}
                 if ops[d]["group"] is not None:

@@ -7,15 +7,20 @@ E = 32768
 SEG = 33
 HALF = SEG * V
 WN = 2 * HALF
-WA = 768
-BW = (256, 512, 512)
+WA = 1280
+BW = (256, 512)
 WB = sum(BW)
-NS = (4, 3)
-NL = 1
+NS = (2,)
+NL = 0
+NV = 0
+PW = 256
+SC = 1
+SK = 0
+SV = 0
 ZP = 1024
-ZH = 12
-ZG = (2048, 2048, 1024, 1280)
-ZV = (1536, 1024, 3072)
+ZH = 15
+ZG = (4096, 2048)
+ZV = (512, 512, 768, 1536, 512)
 KS = 0
 ORDER = "ababababbaba"
 OWN = (0, 8, 24, 64)
@@ -23,16 +28,19 @@ BETWEEN = (4, 1, 1)
 HS = 1
 CG = 64
 ROUND16 = 1.5 * 2 ** 27
-F0 = 304
+F0 = 320
 F1 = 432
 CP = 464
-CL = 448
+TAIL = 1
+FL = 192
+CL = 320
 C0 = 64
 OWN0 = (0, 16, 32, 64)
 BETWEEN0 = (4, 1, 1)
-FA = (0, 1)
+FA = 0
 CUTS = (0, 64, 104, 128, 168, 192)
 AHEAD = 64
+COSTS = (64, 128, 168, 192)
 CUTS0 = (0, 32, 64, 96, 128, 160, 192)
 AHEAD0 = 48
 GV0 = 1
@@ -51,7 +59,7 @@ SCRATCH = {
     "m16": ("sbuf", [128, 128], "bfloat16"), "mm": ("sbuf", [128, 128], "bfloat16"),
     "Bm": ("sbuf", [128, 128], "bfloat16"), "B2": ("sbuf", [128, 128], "bfloat16"), "NB": ("sbuf", [128, 128], "bfloat16"),
     "Im": ("sbuf", [128, 128], "bfloat16"), "N16": ("sbuf", [128, 128], "bfloat16"), "NI": ("sbuf", [128, 128], "bfloat16"),
-    "N64": ("sbuf", [128, 128], "bfloat16"), "dd": ("sbuf", [128, V], "bfloat16"),
+    "BI": ("sbuf", [128, 128], "bfloat16"), "NBI": ("sbuf", [128, 128], "bfloat16"), "N64": ("sbuf", [128, 128], "bfloat16"), "dd": ("sbuf", [128, V], "bfloat16"),
     "TW": ("sbuf", [128, 128], "bfloat16"), "c64": ("sbuf", [128, F0], "bfloat16"),
     "pi": ("sbuf", [128, 8], "int32"), "pf": ("sbuf", [128, 8], "float32"),
     "oh": ("sbuf", [128, 4], "float32"), "jf": ("sbuf", [128, 8], "float32"), "ea": ("sbuf", [128, 8], "float32"),
@@ -74,7 +82,7 @@ SCRATCH = {
     "pR0": ("psum", [128, 1024], "float32"), "pR1": ("psum", [128, 2048], "float32"),
 }
 PART = {"GC": ("SG", 0, 4096), "GV": ("SG", 4096, 4096), "Sel": ("SG", 8192, 512), "cm": ("SG", 8704, 4 * V),
-        "bA": ("SG", 10752, WA), "bB": ("SG", 10752 + WA, WB)}
+        "IK": ("VS1", 0, 2048), "bA": ("SG", 10752, WA), "bB": ("SG", 10752 + WA, WB)}
 POOL = {"v": 44, "s": 32, "t": 16, "g": 8, "y": 22}
 SEMAPHORES = ([q + str(i) for q in POOL for i in range(POOL[q])] + ["ids%d" % t for t in range(3)]
               + ["val%d_%d" % (t, d) for t in range(3) for d in range(3)] + ["li%d" % t for t in range(3)]
@@ -242,12 +250,11 @@ def main_program(g, core, rank, T, topo):
 
     load_costs("s", 0, (0, 1))
     load_costs("y", 0, (2, 3))
-    states = load("y", whole("xi"), T.x0[:])
+    early = load("y", whole("cA"), T.cost[:, 0:16 * WA])
+    load("y", whole("xi"), T.x0[:])
     load("y", whole("d0"), T.drv[:, 0:V + C0])
     load("y", whole("thi"), T.th[:])
     load_costs("y", 1)
-    load("y", whole("cA"), T.cost[:, 0:16 * WA], after=(states,))
-    load_costs("y", 2)
 
     def fan_of(q):
         return R("fanb", V * q, V * q + V)
@@ -256,7 +263,6 @@ def main_program(g, core, rank, T, topo):
         for q in qs:
             load("y", fan_of(q), T.fan[:, V * q:V * q + V])
 
-    load_fan([rank] + peers[:FA[0]])
 
     call("v", g.vector.memset, R("W", 0, ZP), 0.0)
     iota(whole("kf"), [[0, 16], [1, 16]], 0, 0)
@@ -284,7 +290,7 @@ def main_program(g, core, rank, T, topo):
     ts(R("pi", 2, 3), R("pi", 0, 1), 4, A.arith_shift_right)
     ts(R("pi", 3, 4), R("pi", 0, 1), 3, A.bitwise_and)
     ts(R("pi", 4, 5), R("pi", 0, 1), 2, A.arith_shift_right, 7, A.bitwise_and)
-    zero_v(ZV[1])
+    zero_v(256)
     cp(R("pf", 0, 5), R("pi", 0, 5))
     ts(R("pf", 5, 6), R("pi", 1, 2), 0.5, A.add)
     ts(whole("oh"), R("kf", 0, 4), R("pf", 3, 4), A.is_equal)
@@ -292,10 +298,11 @@ def main_program(g, core, rank, T, topo):
     ts(R("jf", 0, 4), R("kf", 0, 4), 16.0, A.mult, R("pf", 5, 6), A.add)
     together("v", (ts(R("Sel", 128 * r, 128 * r + 128), whole("m16"), R("pf", 4, 5), A.is_equal, R("oh", r, r + 1), A.mult)
                    for r in range(4)))
+    zero_v(ZV[1])
 
     def convert(name, a, b):
-        for c in range(a, b, 512):
-            d = min(c + 512, b)
+        for c in range(a, b, PW):
+            d = min(c + PW, b)
             tt(R("b" + name, c, d), R("c" + name, c, d), R("pS", 0, d - c), A.mult)
 
     runs = [(sum(BW[:b]), BW[b], j) for b in range(len(BW)) for j in range(16)]
@@ -428,6 +435,8 @@ def main_program(g, core, rank, T, topo):
             if t and CG < 64 and b == OWN[2]:
                 cost_gather("Uo", 64, CG, 64, 16 * CG)
         theirs = lists(R("id%d" % t, 0, 12), 192, "Er", "Hr", "Ur", 64, "pS")
+        for i in range(6 - sum(between)):
+            next(theirs)
         for (a, b), n in zip(zip(own, own[1:]), between):
             scatter("Uo", a, b, 16 * a)
             for i in range(n):
@@ -438,8 +447,9 @@ def main_program(g, core, rank, T, topo):
         for a, b in zip(cuts, cuts[1:]):
             at, d = 1024 + 16 * a, a // 64
             if done < b:
-                cost_gather("Ur", 192, done, max(b, ahead), 1024 + 16 * done)
-                done = max(b, ahead)
+                upto = [c for c in COSTS if c >= b][0] if t else max(b, ahead)
+                cost_gather("Ur", 192, done, upto, 1024 + 16 * done)
+                done = upto
             value_gather(R(vs, 1024 * d, 1024 * d + 1024), "Ur", 192, a, b, at)
             scatter("Ur", a, b, at)
 
@@ -454,9 +464,19 @@ def main_program(g, core, rank, T, topo):
         return R("pR1", 512 * k + a, 512 * k + b)
 
     convert("B", 0, BW[0])
-    scales("pS", 256)
+    if PW > 256:
+        scales("pS", 256)
     spread_s(1)
     zero_v(ZV[2])
+    convert("A", 0, WA)
+    first = record("y", lambda: g.sync.dma_start(T.CT[0:128:16, 0:16 * WA], ap(whole("bA"))), [whole("bA")], [], dma=True)
+    for b in range(2, len(BW)):
+        load_costs("y", b)
+    load_fan([rank] + peers[:FA])
+    for r in range(1, 16):
+        copied = record("y", (lambda r=r: g.sync.dma_start(T.CT[r:128:16, 0:16 * WA], T.CT[0:128:16, 0:16 * WA])),
+                        [], [], dma=True, fixed=("rep", 16 * 15), after=(first,))
+    zero_v(ZV[4])
     ts(whole("pX"), whole("xi"), -float(DEC), A.add)
     cp(whole("thf"), whole("thi"))
     ts(R("pi", 5, 6), whole("thi"), R("pf", 1, 2), A.add, -1.0, A.add)
@@ -470,58 +490,62 @@ def main_program(g, core, rank, T, topo):
     scan(ff(0, V), whole("ch"), whole("line"), 0.0, A.add, A.max)
     ts(R("jf", 4, 5), R("pi", 1, 2), 16.0, A.mult)
     ts(whole("Im"), whole("mm"), R("pf", 0, 1), A.is_equal)
-    for c in range(4):
+    for c in range(4 - SC):
         ts(R("cm", V * c, V * c + V), ff(0, V), R("jf", c, c + 1), A.is_le, 2.0, A.mult)
-    convert("A", 0, WA)
-    first = record("y", lambda: g.sync.dma_start(T.CT[0:128:16, 0:16 * WA], ap(whole("bA"))), [whole("bA")], [], dma=True)
-    load_fan(peers[FA[0]:FA[1]])
+    spread_s(1)
+    for c in range(4 - SC, 4):
+        act(R("cm", V * c, V * c + V), ff(0, V), F.Sign, bias=R("jf", c, c + 1), scale=-1.0, accum_out=R("ea", 4 + c, 5 + c))
     together("v", (scan(R("GC", 128 * c, 128 * c + 128), R("cm", 256 * c, 256 * c + 128), R("cm", 256 * c + 128, 256 * c + 256),
-                        0.0, A.add, A.add) for c in range(8)))
+                        -256.0, A.add, A.add) for c in range(8 - 2 * SC)))
     ts(R("pi", 6, 7), R("pi", 5, 6), 4, A.arith_shift_right)
     ts(whole("ku"), whole("ki"), R("jf", 4, 5), A.add)
-    tt(R("ea", 4, 8), R("GC", 127, 1024, 256), R("GC", 255, 1024, 256), A.add)
+    tt(R("ea", 4, 8 - SC), R("GC", 127, 1024 - 256 * SC, 256), R("GC", 255, 1024 - 256 * SC, 256), A.add)
     ts(R("pf", 6, 7), R("pi", 6, 7), -1.0, A.mult)
-    spread_s(2)
-    listed(R("ea", 4, 8), 0.5, 0.0)
+    spread_s(1)
+    zero_v(ZV[3])
+    listed(R("ea", 4, 8), 0.5, V / 2.0)
     send_ids(0)
     zero_g(ZG[1])
     convert("B", BW[0] + BW[1], WB)
-    fill_v()
+    if NV:
+        fill_v()
     spread_s(2)
     scaled = {0: ("F64", float(CAP)), 1: ("G64", -float(CAP)), 3: ("F33", float(SEG)), 5: ("NH", -1024.0 * SEG)}
     for i, c in enumerate(values(0)):
-        if i in scaled:
-            later = ts(whole(scaled[i][0]), whole("mm"), R("pf", 0, 1), A.is_equal, scaled[i][1], A.mult)
-        if i == 1:
-            for r in range(1, 16):
-                copied = record("y", (lambda r=r: g.sync.dma_start(T.CT[r:128:16, 0:16 * WA], T.CT[0:128:16, 0:16 * WA])),
-                                [], [], dma=True, fixed=("rep", 16 * 15), after=(first, later))
-            load_fan(peers[FA[1]:])
-    record("g", None, [], [], after=(first,))
-    zero_g(ZG[2])
+        if i in scaled and SK:
+            act(whole(scaled[i][0]), whole("Im"), F.Copy, scale=scaled[i][1])
+        elif i in scaled:
+            ts(whole(scaled[i][0]), whole("mm"), R("pf", 0, 1), A.is_equal, scaled[i][1], A.mult)
     send_values(0)
-    cp(X(whole("Ls"), whole("U")), R("sm", 192, 256))
-    zero_g(ZG[3])
+    record("y", None, [], [], after=(cp(X(whole("Ls"), whole("U")), R("sm", 192, 256)),))
+    load_fan(peers[FA:])
     rest = zend - zpos[0]
-    spread_v()
+    if pending:
+        spread_v()
     mine = lists(whole("U"), 64, "Eo", "Ho", "Uo", 0, "pX")
     for i, n in enumerate(NS):
         spread_s(n)
-        fill_v()
+        if NV > i + 1:
+            fill_v()
         if i == len(NS) - 1:
             spread_s(NL)
             for j in range(4):
                 next(mine)
         zero_v(rest // len(NS) // 16 * 16 if i < len(NS) - 1 else zend - zpos[0])
-        spread_v()
+        if pending:
+            spread_v()
     spread_s(len(runs))
     for c in mine:
         pass
     ts(R("xb", 0, C0), R("d0", V, V + C0), 1.0, A.add)
-    cp(R("GV", 0, 16 * OWN0[GV0]), X(whole("VO"), R("Uo", 64, 64 + OWN0[GV0])))
+    if SV:
+        value_gather(whole("VO"), "Uo", 64, 0, OWN0[GV0], 0)
+    else:
+        cp(R("GV", 0, 16 * OWN0[GV0]), X(whole("VO"), R("Uo", 64, 64 + OWN0[GV0])))
     record("s", None, [], [], after=(copied,))
     tt(cells(1, 0, C0), R("xb", 0, C0), R("pS", 0, C0), A.mult)
-    later = tt(cells(0, 0, V), whole("xa"), whole("pS"), A.mult)
+    for a in range(0, V, PW):
+        later = tt(cells(0, a, a + PW), R("xa", a, a + PW), R("pS", 0, PW), A.mult)
     load("y", R("dr", 0, V), T.drv[:, V:2 * V], after=(later,))
     items(0)
     load("y", R("dr", V, 3 * V), T.drv[:, 2 * V:RO * V], after=(len(ops) - 7,))
@@ -538,7 +562,7 @@ def main_program(g, core, rank, T, topo):
         return R("SG", SEG * a + SEG - 1, SEG * b, SEG)
 
     def sums(a, b):
-        return R("pR0", a, b) if a < F0 else R("pR0", 512 + a, 512 + b) if a < F1 else R("pS", a - F1, b - F1)
+        return R("pR0", a, b) if a == 0 else R("pR0", 512 + a, 512 + b) if a < F1 else R("pS", a - F1, b - F1)
 
     def differ(a, b):
         summed(bank(0, a, b), ("NI", R("Ls", a, b)), ("Im", view(a, b)))
@@ -571,9 +595,9 @@ def main_program(g, core, rank, T, topo):
             tt(R("mx", a, b), view(a, b), R("Ls", a, b), A.max)
         summed(sums(F1, V), ("TW", R("St", F1, V)), ("NB", R("Ls", F1, V)), ("NB", view(F1, V)), ("B2", R("mx", F1, V)))
 
-    def last_marks(run):
-        ts(R("ch", F0, F1), sums(F0, F1), 0.0, A.is_gt)
-        run(F0, F1)
+    def last_marks(run, a):
+        ts(R("ch", a, F1), sums(a, F1), 0.0, A.is_gt)
+        run(a, F1)
         ts(R("ch", F1, V), sums(F1, V), 0.0, A.is_gt)
         run(F1, V)
 
@@ -595,29 +619,42 @@ def main_program(g, core, rank, T, topo):
     def capped(a, b):
         scan(ff(a, b), R("ch", a, b), R("c64", 0, b - a), ff(a - 1, a), A.add, A.min)
 
-    def stepped(a, b):
-        summed(bank(3, a, b), ("Im", ff(a, b)), ("NI", ff(a - 1, b - 1)))
+    def unscaled(name, first, step):
+        together("t", (mm(R("pX", k, FL, 16), R("IK", 128 * k, 128 * k + 128),
+                          R(name, first + step * k, step * FL, 16 * step), True, True) for k in range(16)))
 
-    def gated(a, b):
-        tt(R("mx", a, b), bank(3, a, b), R("dd", a, b), A.mult)
-        summed(bank(1, a, b), ("Im", R("Ls", a, b)), ("NI", R("St", a, b)), ("Im", R("mx", a, b)))
+    def old_last():
+        unscaled("Ls", 0, 1)
+        act(R("dS", 0, FL), R("pX", 0, FL), F.Copy)
 
-    def out_l(a, b):
-        tt(R("lo", a, b), bank(1, a, b), R("xb", a, b), A.mult)
-        outs.append(store("y", T.yl[:, a:b], R("lo", a, b)))
+    def first_x():
+        unscaled("SG", SEG - 1, SEG)
+        act(R("dd", 0, FL), R("pX", 0, FL), F.Identity, bias=-256.0)
+        act(R("xo", 0, FL), R("pX", 0, FL), F.Identity, bias=-1.0)
+        outs.append(store("y", T.yx[:, 0:FL], R("xo", 0, FL)))
 
-    def lowered(a, b):
-        summed(bank(2, a, b), ("Im", view(a, b)), ("NI", R("St", a, b)))
+    def gate():
+        summed(bank(2, 0, FL), ("BI", ff(0, FL)), ("NBI", ff(-1, FL - 1)), ("Im", R("dd", 0, FL)))
+        summed(bank(2, FL, 2 * FL), ("NBI", ff(0, FL)), ("BI", ff(-1, FL - 1)), ("Im", R("dS", 0, FL)))
 
-    def out_x(a, b):
-        tt(R("xo", a, b), bank(2, a, b), R("xb", a, b), A.mult)
-        outs.append(store("s", T.yx[:, a:b], R("xo", a, b)))
+    def first_last():
+        act(R("cl", 0, 2 * FL), bank(2, 0, 2 * FL), F.Relu)
+        summed(R("pR0", 0, FL), ("Im", R("cl", 0, FL)), ("Im", R("cl", FL, 2 * FL)))
+        act(R("lo", 0, FL), R("pR0", 0, FL), F.Identity, bias=-1.0)
+        outs.append(store("y", T.yl[:, 0:FL], R("lo", 0, FL)))
+
+    def lowered(out, a, b):
+        summed(out, ("Im", view(a, b)), ("NI", R("St", a, b)))
 
     def last_constants():
         act(whole("xb"), whole("iS0"), F.Copy, scale=2.0 ** 64)
         act(whole("c64"), R("line", 0, F0), F.Identity, bias=float(CAP), scale=0.0)
         act(ff(-1, 0), R("kf", 0, 1), F.Copy)
-        act(whole("N64"), whole("Im"), F.Copy, scale=-1.0 / CAP)
+        for name, k in (("N64", -1.0 / CAP), ("BI", 256.0), ("NBI", -256.0)):
+            act(whole(name), whole("Im"), F.Copy, scale=k)
+        act(R("IK", 0, 128), whole("Im"), F.Copy, scale=2.0 ** 64)
+        for n in (1, 2, 4, 8):
+            act(R("IK", 128 * n, 256 * n), R("IK", 0, 128 * n), F.Copy, scale=2.0 ** (-8 * n))
 
     def do(*calls):
         return [(c[0], c[1:]) for c in calls]
@@ -641,7 +678,7 @@ def main_program(g, core, rank, T, topo):
                 V - 16: [], V: do((last_sums,), (differ, F1, V), (fallen, 2, F0, V))}
         plan[CP] = plan.get(CP, []) + do((count, 0, F0), *[(before, c) for c in range(4)])
         scans(t, plan)
-        last_marks(count)
+        last_marks(count, F0)
         choose()
         send_ids(t)
         kept(F0, V)
@@ -650,20 +687,54 @@ def main_program(g, core, rank, T, topo):
         own_lists(t)
         items(t)
 
-    plan = {F0: do((differ, 0, F0), (lowered, 0, F0), (summed_abs, 0, F0), (kept, 0, F0), (mark, 0, F0)),
-            F0 + 48: do((out_x, 0, F0)),
-            F1: do((differ, F0, F1), (summed_abs, F0, F1)),
-            V - 16: do((gated, 0, F0)),
-            V: do((last_sums,), (differ, F1, V), (lowered, F0, V), (out_l, 0, F0))}
-    plan[CL] = plan.get(CL, []) + do((capped, 0, F0), (stepped, 0, F0))
-    scans(RO - 1, plan)
-    last_marks(capped)
-    summed(bank(3, F0, V), ("N64", R("c64", 0, FW)), ("Im", ff(F0, V)), ("NI", ff(F0 - 1, V - 1)))
-    out_x(F0, V)
-    tt(R("acc", 0, FW), bank(0, F0, V), R("xb", F0, V), A.mult)
-    tt(R("pX", 0, FW), bank(3, F0, V), R("acc", 0, FW), A.mult)
-    tt(R("lo", F0, V), R("pX", 0, FW), R("xo", F0, V), A.add)
-    outs.append(store("y", T.yl[:, F0:V], R("lo", F0, V)))
+    def stepped():
+        summed(bank(3, 0, FL), ("Im", ff(0, FL)), ("NI", ff(-1, FL - 1)))
+
+    def gated():
+        tt(R("mx", 0, FL), bank(3, 0, FL), R("dd", 0, FL), A.mult)
+        summed(R("pR0", 0, FL), ("Im", R("Ls", 0, FL)), ("NI", R("St", 0, FL)), ("Im", R("mx", 0, FL)))
+
+    def out_l():
+        tt(R("lo", 0, FL), R("pR0", 0, FL), R("xb", 0, FL), A.mult)
+        outs.append(store("y", T.yl[:, 0:FL], R("lo", 0, FL)))
+
+    def out_x():
+        tt(R("xo", 0, FL), bank(2, 0, FL), R("xb", 0, FL), A.mult)
+        outs.append(store("y", T.yx[:, 0:FL], R("xo", 0, FL)))
+
+    if TAIL:
+        old_last()
+        scans(RO - 1, {FL: do((differ, 0, FL), (summed_abs, 0, FL), (mark, 0, FL), (first_x,)),
+                       CL: do((capped, 0, FL), (gate,)),
+                       F1: do((differ, FL, F1), (summed_abs, FL, F1), (lowered, bank(1, 0, F1 - FL), FL, F1), (first_last,)),
+                       V - 16: [], V: do((last_sums,))})
+    else:
+        plan = {FL: do((differ, 0, FL), (lowered, bank(2, 0, FL), 0, FL), (summed_abs, 0, FL), (kept, 0, FL), (mark, 0, FL)),
+                FL + 48: do((out_x,)),
+                F1: do((differ, FL, F1), (summed_abs, FL, F1), (lowered, bank(2, 0, F1 - FL), FL, F1)),
+                V - 16: do((gated,)), V: do((last_sums,), (out_l,))}
+        plan[CL] = plan.get(CL, []) + do((capped, 0, FL), (stepped,))
+        scans(RO - 1, plan)
+    d_end, x_end = R("pX", 256, 256 + V - F1), R("pX", 384, 384 + V - F1)
+    summed(d_end, ("NI", R("Ls", F1, V)), ("Im", view(F1, V)))
+    lowered(x_end, F1, V)
+    ts(R("ch", FL, F1), sums(FL, F1), 0.0, A.is_gt)
+    tt(R("acc", FL, F1), bank(0, FL, F1), R("xb", FL, F1), A.mult)
+    parts = ((3, FL, F1), (1, F1, V))
+    for k, a, b in parts:
+        if a == F1:
+            ts(R("ch", F1, V), sums(F1, V), 0.0, A.is_gt)
+            tt(R("xo", FL, F1), bank(1 if TAIL else 2, 0, F1 - FL), R("xb", FL, F1), A.mult)
+        capped(a, b)
+        summed(bank(k, a, b), ("N64", R("c64", 0, b - a)), ("Im", ff(a, b)), ("NI", ff(a - 1, b - 1)))
+    tt(R("xo", F1, V), x_end, R("xb", F1, V), A.mult)
+    outs.append(store("s", T.yx[:, FL:V], R("xo", FL, V)))
+    tt(R("acc", F1, V), d_end, R("xb", F1, V), A.mult)
+    for k, a, b in parts:
+        tt(R("pX", a - FL, b - FL), bank(k, a, b), R("acc", a, b), A.mult)
+    for k, a, b in parts:
+        tt(R("lo", a, b), R("pX", a - FL, b - FL), R("xo", a, b), A.add)
+    outs.append(store("y", T.yl[:, FL:V], R("lo", FL, V)))
     record("y", None, [], [], after=outs)
 
     known = {q: set() for q in Q}

import math
from concourse.bass import DstId, RemoteDMATransfer
from concourse.mybir import AluOpType, ActivationFunctionType

V, CAP, RO, DEC, NR = 512, 64, 4, 16, 4
E = 32768
SEG = 33
HALF = SEG * V
WN = 2 * HALF
WA = 1280
BW = (256, 512)
WB = sum(BW)
NS = (2,)
NL = 0
NV = 0
PW = 256
SC = 1
SK = 0
SV = 0
ZP = 1024
ZH = 15
ZG = (4096, 2048)
ZV = (512, 512, 768, 1536, 512)
KS = 0
ORDER = "ababababbaba"
OWN = (0, 8, 24, 64)
BETWEEN = (4, 1, 1)
HS = 1
CG = 64
ROUND16 = 1.5 * 2 ** 27
F0 = 320
F1 = 432
CP = 464
TAIL = 1
FL = 192
CL = 320
C0 = 64
OWN0 = (0, 16, 32, 64)
BETWEEN0 = (4, 1, 1)
FA = 0
CUTS = (0, 64, 104, 128, 168, 192)
AHEAD = 64
COSTS = (64, 128, 168, 192)
CUTS0 = (0, 32, 64, 96, 128, 160, 192)
AHEAD0 = 48
GV0 = 1
GV1 = 0
FW = V - F0
LN2 = math.log(2.0)

SCRATCH = {
    "W": ("sbuf", [128, WN], "bfloat16"), "CT": ("sbuf", [128, E], "bfloat16"), "SG": ("sbuf", [128, HALF], "bfloat16"),
    "fanb": ("sbuf", [128, 2048], "int32"), "cA": ("sbuf", [128, WA], "int32"), "cB": ("sbuf", [128, WB], "int32"),
    "xi": ("sbuf", [128, V], "int32"), "d0": ("sbuf", [128, V + C0], "int32"), "dr": ("sbuf", [128, 3 * V], "int32"),
    "thi": ("sbuf", [128, 1], "int32"), "thf": ("sbuf", [128, 1], "float32"),
    "VS0": ("sbuf", [128, 3072], "bfloat16"), "VS1": ("sbuf", [128, 3072], "bfloat16"),
    "VO": ("sbuf", [128, 1024], "bfloat16"),
    "kf": ("sbuf", [128, 256], "bfloat16"), "line": ("sbuf", [128, V], "bfloat16"),
    "m16": ("sbuf", [128, 128], "bfloat16"), "mm": ("sbuf", [128, 128], "bfloat16"),
    "Bm": ("sbuf", [128, 128], "bfloat16"), "B2": ("sbuf", [128, 128], "bfloat16"), "NB": ("sbuf", [128, 128], "bfloat16"),
    "Im": ("sbuf", [128, 128], "bfloat16"), "N16": ("sbuf", [128, 128], "bfloat16"), "NI": ("sbuf", [128, 128], "bfloat16"),
    "BI": ("sbuf", [128, 128], "bfloat16"), "NBI": ("sbuf", [128, 128], "bfloat16"), "N64": ("sbuf", [128, 128], "bfloat16"), "dd": ("sbuf", [128, V], "bfloat16"),
    "TW": ("sbuf", [128, 128], "bfloat16"), "c64": ("sbuf", [128, F0], "bfloat16"),
    "pi": ("sbuf", [128, 8], "int32"), "pf": ("sbuf", [128, 8], "float32"),
    "oh": ("sbuf", [128, 4], "float32"), "jf": ("sbuf", [128, 8], "float32"), "ea": ("sbuf", [128, 8], "float32"),
    "St": ("sbuf", [128, V], "bfloat16"), "Ls": ("sbuf", [128, V], "bfloat16"), "iS0": ("sbuf", [128, V], "bfloat16"),
    "xs": ("sbuf", [128, V], "bfloat16"), "mx": ("sbuf", [128, V], "bfloat16"), "ch": ("sbuf", [128, V], "bfloat16"),
    "ff": ("sbuf", [128, V + 16], "bfloat16"), "xa": ("sbuf", [128, V], "bfloat16"), "xb": ("sbuf", [128, V], "bfloat16"),
    "jk": ("sbuf", [128, F0], "bfloat16"), "cl": ("sbuf", [128, 4 * FW], "bfloat16"),
    "dS": ("sbuf", [128, V], "bfloat16"), "acc": ("sbuf", [128, 1024], "float32"),
    "U": ("sbuf", [128, 4], "uint16"), "ido": ("sbuf", [128, 4], "uint16"),
    "id0": ("sbuf", [128, 16], "uint16"), "id1": ("sbuf", [128, 16], "uint16"), "id2": ("sbuf", [128, 16], "uint16"),
    "Eo": ("sbuf", [128, 128], "float32"), "Er": ("sbuf", [128, 384], "float32"),
    "F64": ("sbuf", [128, 128], "float32"), "G64": ("sbuf", [128, 128], "float32"), "F33": ("sbuf", [128, 128], "float32"),
    "NH": ("sbuf", [128, 128], "bfloat16"),
    "Jb": ("sbuf", [128, 192], "bfloat16"), "ki": ("sbuf", [128, 32], "int32"), "ku": ("sbuf", [128, 32], "uint16"),
    "Ho": ("sbuf", [128, 64], "bfloat16"), "Hr": ("sbuf", [128, 192], "bfloat16"),
    "Uo": ("sbuf", [128, 192], "uint16"), "Ur": ("sbuf", [128, 576], "uint16"),
    "sm": ("sbuf", [128, 256], "bfloat16"),
    "xo": ("sbuf", [128, V], "float32"), "lo": ("sbuf", [128, V], "float32"),
    "pS": ("psum", [128, 512], "float32"), "pX": ("psum", [128, 512], "float32"),
    "pR0": ("psum", [128, 1024], "float32"), "pR1": ("psum", [128, 2048], "float32"),
}
PART = {"GC": ("SG", 0, 4096), "GV": ("SG", 4096, 4096), "Sel": ("SG", 8192, 512), "cm": ("SG", 8704, 4 * V),
        "IK": ("VS1", 0, 2048), "bA": ("SG", 10752, WA), "bB": ("SG", 10752 + WA, WB)}
POOL = {"v": 44, "s": 32, "t": 16, "g": 8, "y": 22}
SEMAPHORES = ([q + str(i) for q in POOL for i in range(POOL[q])] + ["ids%d" % t for t in range(3)]
              + ["val%d_%d" % (t, d) for t in range(3) for d in range(3)] + ["li%d" % t for t in range(3)]
              + ["lv%d" % t for t in range(3)] + ["zin", "zout", "zarr", "rep"])
A = AluOpType
F = ActivationFunctionType


def R(name, lo, hi, step=1, rows=(0, 128)):
    if name in PART:
        return ("R", PART[name][0], PART[name][1] + lo, PART[name][1] + hi, step, rows)
    return ("R", name, lo, hi, step, rows)


def whole(name):
    return R(name, 0, PART[name][2] if name in PART else SCRATCH[name][1][1])


def X(win, off):
    return ("X", win, off)


def helper_of(core, T, topo):
    free = [c for c in topo.cores_of(core) if T.rank_of(c) is None]
    out = {}
    for r in T.cores:
        out[r] = [c for c in free if topo.die(c) == topo.die(r) and c not in out.values()][0]
    return out


def rank_program(g, core, T, topo):
    rank = T.rank_of(core)
    if rank is not None:
        main_program(g, core, rank, T, topo)
    elif topo.chip(core) == topo.chip(T.cores[0]):
        for r, h in helper_of(core, T, topo).items():
            if h == core:
                helper_program(g, core, r, T, topo)


def helper_program(g, core, dst, T, topo):
    n = len(topo.engines(core, dst))
    rid, pid = topo.addr(dst)[:2]
    g.wait_ge(T.sem.zin, len(topo.engines(dst, core)))
    g.remote_dma_fused([RemoteDMATransfer(
        dst_ids=[DstId(rid=rid, pnc=pid) for k in range(ZH)], dma_engine_mask=topo.mask(core, dst), remote_sem=T.sem.zarr,
        srcs=[T.W[:, 0:ZP]], dsts=[T.W[:, WN - (k + 1) * ZP:WN - k * ZP] for k in range(ZH)])], local_sem=T.sem.zout)
    g.wait_ge(T.sem.zout, n)


def main_program(g, core, rank, T, topo):
    Q = {"v": g.vector, "s": g.scalar, "t": g.tensor, "g": g, "y": g.sync}
    ops = []
    acc = {}
    group = [None, None]

    def together(q, calls, name=None):
        group[0], group[1] = name or len(ops), q
        for c in calls:
            pass
        group[0] = group[1] = None

    def ap(a):
        if isinstance(a, tuple) and a[0] == "R":
            return T[a[1]][a[5][0]:a[5][1], a[2]:a[3]] if a[4] == 1 else T[a[1]][a[5][0]:a[5][1], a[2]:a[3]:a[4]]
        if isinstance(a, tuple) and a[0] == "X":
            return ap(a[1]).indirect(ap(a[2]))
        return a

    def record(q, fn, reads, writes, dma=False, fixed=None, after=()):
        me = len(ops)
        deps = set(after)
        grp = group[0] if q == group[1] else None
        touch = [(r, False) for r in reads] + [(r, True) for r in writes]
        for r, wr in touch:
            name, lo, hi = r[1:4]
            ps = SCRATCH[name][0] == "psum"
            for (l2, h2, o2, w2) in acc.get(name, []):
                if ps and ops[o2]["q"] != q:
                    if l2 // 512 <= (hi - 1) // 512 and lo // 512 <= (h2 - 1) // 512:
                        deps.add(o2)
                elif grp is not None and ops[o2]["group"] == grp:
                    continue
                elif l2 < hi and lo < h2 and (w2 or wr) and not (ps and q == "t"):
                    deps.add(o2)
        for r, wr in touch:
            acc.setdefault(r[1], []).append((r[2], r[3], me, wr))
        ops.append({"q": q, "fn": fn, "deps": deps, "dma": dma, "fixed": fixed, "group": grp})
        return me

    def call(q, fn, *args, **kw):
        reads, writes = [], []
        for i, a in enumerate(list(args) + [kw[k] for k in kw if k != "accum_out"]):
            if isinstance(a, tuple) and a[0] == "R":
                (writes if i == 0 else reads).append(a)
            elif isinstance(a, tuple) and a[0] == "X":
                (writes if i == 0 else reads).append(a[1])
                reads.append(a[2])
        if "accum_out" in kw:
            writes.append(kw["accum_out"])
        return record(q, lambda: fn(*[ap(a) for a in args], **{k: ap(kw[k]) for k in kw}), reads, writes)

    def ts(out, in0, s1, op0, s2=None, op1=None):
        if op1 is None:
            return call("v", g.vector.tensor_scalar, out, in0, s1, None, op0)
        return call("v", g.vector.tensor_scalar, out, in0, s1, s2, op0, op1)

    def tt(out, in0, in1, op):
        return call("v", g.vector.tensor_tensor, out, in0, in1, op)

    def cp(out, in_):
        return call("v", g.vector.tensor_copy, out, in_)

    def scan(out, d0, d1, first, op0, op1):
        return call("v", g.vector.tensor_tensor_scan, out, d0, d1, first, op0, op1)

    def act(out, in_, func, **kw):
        return call("s", g.scalar.activation, out, in_, func, **kw)

    def mm(out, lhsT, rhs, start, stop):
        return call("t", g.tensor.matmul, out, lhsT, rhs, start, stop)

    def summed(out, *terms):
        together("t", (mm(out, whole(lhsT), rhs, i == 0, i == len(terms) - 1) for i, (lhsT, rhs) in enumerate(terms)))

    def iota(out, pattern, base, cm):
        if SCRATCH[out[1]][2] == "int32":
            return call("g", g.iota, out, pattern, base, cm)
        return call("g", g.iota, out, pattern, base, cm, allow_small_or_imprecise_dtypes=True)

    def load(q, out, src, after=()):
        return record(q, lambda: Q[q].dma_start(ap(out), src), [], [out], dma=True, after=after)

    def store(q, dst, src):
        return record(q, lambda: Q[q].dma_start(dst, ap(src)), [src], [], dma=True)

    def arrival(sem, count, writes):
        return record(None, None, [], writes, dma=True, fixed=(sem, count))

    def peers_of(r):
        c = T.cores[r]
        return sorted([q for q in range(NR) if q != r], key=lambda q: (topo.die(T.cores[q]) != topo.die(c), q ^ r))
    peers = peers_of(rank)
    slot = {q: peers_of(q).index(rank) for q in peers}
    mask = topo.mask(core, T.cores[peers[0]])
    neng = len(topo.engines(core, T.cores[peers[0]]))
    helper = helper_of(core, T, topo)[core]

    zend = WN - ZH * ZP - sum(ZG)
    zpos = [ZP, zend]

    def zero_v(n):
        together("v", (call("v", g.vector.memset, R("W", a, a + n), 0.0) for a in zpos[:1]), "zv")
        zpos[0] += n

    def zero_g(n):
        together("g", (iota(R("W", a, a + n), [[0, n]], 0, 0) for a in zpos[1:]), "zg")
        zpos[1] += n

    def load_costs(q, b, quarters=range(4)):
        w, c0 = BW[b], sum(BW[:b])
        e0 = 16 * (WA + c0)
        together(q, (load(q, R("cB", c0, c0 + w, 1, (32 * a, 32 * a + 32)), T.cost[:, e0 + 4 * w * a:e0 + 4 * w * (a + 1)])
                     for a in quarters), ("costs", b))

    load_costs("s", 0, (0, 1))
    load_costs("y", 0, (2, 3))
    early = load("y", whole("cA"), T.cost[:, 0:16 * WA])
    load("y", whole("xi"), T.x0[:])
    load("y", whole("d0"), T.drv[:, 0:V + C0])
    load("y", whole("thi"), T.th[:])
    load_costs("y", 1)

    def fan_of(q):
        return R("fanb", V * q, V * q + V)

    def load_fan(qs):
        for q in qs:
            load("y", fan_of(q), T.fan[:, V * q:V * q + V])


    call("v", g.vector.memset, R("W", 0, ZP), 0.0)
    iota(whole("kf"), [[0, 16], [1, 16]], 0, 0)
    iota(R("pi", 0, 1), [[0, 1]], 0, 1)
    iota(whole("m16"), [[1, 8], [0, 16]], 0, 0)
    hr, hp = topo.addr(helper)[:2]
    record("g", lambda: g.remote_dma(T.W[:, 0:ZP], T.W[:, 0:ZP], T.sem.zin, T.sem.zout, hp, hr, topo.mask(core, helper)),
           [R("W", 0, ZP)], [], dma=True, fixed=("zout", len(topo.engines(core, helper))))
    arrival("zarr", ZH * len(topo.engines(helper, core)), [R("W", WN - ZH * ZP, WN)])
    iota(whole("line"), [[1, V]], CAP + 1 - V, 0)
    iota(whole("Jb"), [[0, 3], [1, 64]], 0, 0)
    iota(whole("ki"), [[1, 16], [256, 2]], 0, 0)
    iota(whole("mm"), [[1, 128]], 0, 0)
    zero_g(ZG[0])

    def scales(name, h):
        act(R(name, h, h + 256), whole("kf"), F.Exp, bias=-64 * LN2, scale=8 * LN2)

    scales("pS", 0)
    scales("Ls", 0)
    scales("Ls", 256)

    zero_v(ZV[0])
    ts(R("pi", 1, 2), R("pi", 0, 1), 15, A.bitwise_and)
    ts(R("pi", 2, 3), R("pi", 0, 1), 4, A.arith_shift_right)
    ts(R("pi", 3, 4), R("pi", 0, 1), 3, A.bitwise_and)
    ts(R("pi", 4, 5), R("pi", 0, 1), 2, A.arith_shift_right, 7, A.bitwise_and)
    zero_v(256)
    cp(R("pf", 0, 5), R("pi", 0, 5))
    ts(R("pf", 5, 6), R("pi", 1, 2), 0.5, A.add)
    ts(whole("oh"), R("kf", 0, 4), R("pf", 3, 4), A.is_equal)
    ts(whole("Bm"), whole("m16"), R("pf", 2, 3), A.is_equal)
    ts(R("jf", 0, 4), R("kf", 0, 4), 16.0, A.mult, R("pf", 5, 6), A.add)
    together("v", (ts(R("Sel", 128 * r, 128 * r + 128), whole("m16"), R("pf", 4, 5), A.is_equal, R("oh", r, r + 1), A.mult)
                   for r in range(4)))
    zero_v(ZV[1])

    def convert(name, a, b):
        for c in range(a, b, PW):
            d = min(c + PW, b)
            tt(R("b" + name, c, d), R("c" + name, c, d), R("pS", 0, d - c), A.mult)

    runs = [(sum(BW[:b]), BW[b], j) for b in range(len(BW)) for j in range(16)]
    piece = [16 * WA, 0, 0, 0, 0]
    pending = []

    def select(pr, p0, n):
        a = piece[0]
        b = piece[0] = min(a + n, E)
        c = a
        group[0], group[1] = len(ops), "t"
        while c < b:
            c0, w, j = runs[piece[2]]
            o = piece[3]
            k = min(w - o, 512 - (c - a) % 512, b - c)
            rows = (32 * (j // 4), 32 * (j // 4) + 32)
            mm(R(pr, p0 + c - a, p0 + c - a + k), R("Sel", 128 * (j % 4), 128 * (j % 4) + 128, 1, rows),
               R("bB", c0 + o, c0 + o + k, 1, rows), True, True)
            c += k
            piece[2], piece[3] = (piece[2] + 1, 0) if o + k == w else (piece[2], o + k)
        group[0] = group[1] = None
        return R("CT", a, b), R(pr, p0, p0 + b - a)

    def spread_s(n):
        for j in range(n):
            if piece[0] < E:
                piece[1] += 1
                act(*select("pR1", 1024 * (piece[1] % 2), 1024), F.Copy)

    def fill_v():
        pending.append(select("pR0", 0, 1024))

    def spread_v():
        cp(*pending.pop(0))

    def ff(a, b):
        return R("ff", 16 + a, 16 + b)

    def listed(last, k, base):
        ts(whole("U"), last, k, A.mult, base, A.add)
        ts(whole("ido"), last, k, A.mult, base + V * rank, A.add)

    def lists(ids, n, e, h, u, px, pc):
        y, y16, hi = R(e, 0, n), R(e, n, 2 * n), R(h, 0, n)
        place, cell = R("pX", px, px + n), R(pc, 256 + px, 256 + px + n)
        if n == CAP:
            yield cp(R(u, 2 * n, 3 * n), X(fan_of(rank), ids))
            yield ts(y, X(fan_of(rank), ids), -7.5, A.add)
        else:
            yield ts(y, X(whole("fanb"), ids), -7.5, A.add)
            yield ts(R(u, 2 * n, 3 * n), y, 7.75, A.add)
        ts(y16, y, ROUND16, A.add, ROUND16, A.subtract)
        yield summed(place, ("Im", R("Jb", 0, n)), ("F64", y), ("G64", y16))
        if n == CAP or not HS:
            ts(hi, y, 1.0 / 1024, A.mult, 159.5078, A.add)
        else:
            act(hi, y, F.Identity, scale=1.0 / 1024, bias=159.5078)
        yield summed(cell, ("F33", y), ("NH", hi), ("Im", hi))
        yield ts(R(u, n, 2 * n), place, 7.5 * CAP + 0.25, A.add)
        yield ts(R(u, 0, n), cell, 7.5 * SEG + 160.0 * (1024 * SEG - 1), A.add, 0.25, A.add)

    def values(t):
        U = whole("U")
        if t:
            yield cp(R("sm", 0, 64), X(whole("ch"), U))
            yield tt(R("sm", 64, 128), X(whole("dd"), U), R("sm", 0, 64), A.mult)
            yield tt(R("sm", 192, 256), X(whole("Ls"), U), R("sm", 64, 128), A.add)
            yield tt(R("VO", 0, 64), X(whole("iS0"), U), R("sm", 192, 256), A.mult)
        else:
            yield cp(R("sm", 0, 64), X(whole("mx"), U))
            yield tt(R("sm", 64, 128), X(whole("ch"), U), R("sm", 0, 64), A.mult)
            yield ts(R("sm", 128, 192), R("sm", 64, 128), 1.0, A.add)
            yield ts(R("VO", 0, 64), R("sm", 64, 128), 1.0, A.add, 2.0 ** -64, A.mult)
            yield tt(R("sm", 192, 256), X(whole("Ls"), U), R("sm", 128, 192), A.mult)
        yield together("v", (ts(R("VO", 64 * k, 64 * k + 64), R("VO", 0, 64), 2.0 ** (8 * k), A.mult) for k in (1, 2, 3)))
        for k in (1, 2, 3):
            if k > KS or not t:
                ts(R("VO", 256 * k, 256 * k + 256), R("VO", 0, 256), 2.0 ** (32 * k), A.mult)
            else:
                act(R("VO", 256 * k, 256 * k + 256), R("VO", 0, 256), F.Copy, scale=2.0 ** (32 * k))
        yield

    def send_ids(t):
        idt = "id%d" % t
        tr = RemoteDMATransfer(
            dst_ids=[DstId(rid=topo.addr(T.cores[q])[0], pnc=topo.addr(T.cores[q])[1]) for q in peers],
            dma_engine_mask=mask, remote_sem=T.sem["ids%d" % t], srcs=[T.ido[:]],
            dsts=[T[idt][:, 4 * slot[q]:4 * slot[q] + 4] for q in peers])
        record("g", lambda: g.remote_dma_fused([tr], local_sem=T.sem["li%d" % t]), [whole("ido")], [], dma=True,
               fixed=("li%d" % t, neng))
        arrival("ids%d" % t, 3 * neng, [R(idt, 0, 12)])

    def send_values(t):
        vs = "VS%d" % (t % 2)
        for q in peers:
            rid, pid = topo.addr(T.cores[q])[:2]
            record("g", (lambda q=q, rid=rid, pid=pid: g.remote_dma(
                T[vs][:, 1024 * slot[q]:1024 * slot[q] + 1024], T.VO[:], T.sem["val%d_%d" % (t, slot[q])],
                T.sem["lv%d" % t], pid, rid, mask)), [whole("VO")], [], dma=True, fixed=("lv%d" % t, 3 * neng))
        for d in range(3):
            arrival("val%d_%d" % (t, d), neng, [R(vs, 1024 * d, 1024 * d + 1024)])

    def cost_gather(u, n, a, b, at):
        act(R("GC", at, at + 16 * (b - a)), X(whole("CT"), R(u, 2 * n + a, 2 * n + b)), F.Identity, scale=-1.0)

    def value_gather(win, u, n, a, b, at):
        act(R("GV", at, at + 16 * (b - a)), X(win, R(u, n + a, n + b)), F.Identity)

    def own_lists(t):
        a, b = lists(whole("U"), 64, "Eo", "Ho", "Uo", 0, "pS"), values(t)
        for i, who in enumerate(ORDER):
            next(a if who == "a" else b)
            if i == 0:
                cost_gather("Uo", 64, 0, CG, 0)
            if i == ORDER.rindex("b"):
                send_values(t)
        cp(X(whole("Ls"), whole("U")), R("sm", 192, 256))

    def scatter(u, a, b, at):
        w = 16 * (b - a)
        return tt(X(whole("W"), R(u, a, b)), R("GC", at, at + w), R("GV", at, at + w), A.add)

    def items(t):
        own, between = (OWN, BETWEEN) if t else (OWN0, BETWEEN0)
        for a, b in zip(own, own[1:]):
            if not t:
                cost_gather("Uo", 64, a, b, 16 * a)
            if t or a >= own[GV0]:
                value_gather(whole("VO"), "Uo", 64, a, b, 16 * a)
            if t and CG < 64 and b == OWN[2]:
                cost_gather("Uo", 64, CG, 64, 16 * CG)
        theirs = lists(R("id%d" % t, 0, 12), 192, "Er", "Hr", "Ur", 64, "pS")
        for i in range(6 - sum(between)):
            next(theirs)
        for (a, b), n in zip(zip(own, own[1:]), between):
            scatter("Uo", a, b, 16 * a)
            for i in range(n):
                next(theirs)
        vs = "VS%d" % (t % 2)
        done = 0
        cuts, ahead = (CUTS, AHEAD) if t else (CUTS0, AHEAD0)
        for a, b in zip(cuts, cuts[1:]):
            at, d = 1024 + 16 * a, a // 64
            if done < b:
                upto = [c for c in COSTS if c >= b][0] if t else max(b, ahead)
                cost_gather("Ur", 192, done, upto, 1024 + 16 * done)
                done = upto
            value_gather(R(vs, 1024 * d, 1024 * d + 1024), "Ur", 192, a, b, at)
            scatter("Ur", a, b, at)

    def scaled_drive(t):
        together("s", (act(R("dS", k, V, 16), X(R("dr", V * (t - 1), V * t), R("ku", 2 * k, 2 * k + 2)), F.Identity,
                           bias=2.0 ** (8 * k - 64), scale=2.0 ** (8 * k - 64)) for k in range(16)))

    def cells(half, a, b):
        return R("W", half * HALF + SEG * a + SEG - 1, half * HALF + SEG * b, SEG)

    def bank(k, a, b):
        return R("pR1", 512 * k + a, 512 * k + b)

    convert("B", 0, BW[0])
    if PW > 256:
        scales("pS", 256)
    spread_s(1)
    zero_v(ZV[2])
    convert("A", 0, WA)
    first = record("y", lambda: g.sync.dma_start(T.CT[0:128:16, 0:16 * WA], ap(whole("bA"))), [whole("bA")], [], dma=True)
    for b in range(2, len(BW)):
        load_costs("y", b)
    load_fan([rank] + peers[:FA])
    for r in range(1, 16):
        copied = record("y", (lambda r=r: g.sync.dma_start(T.CT[r:128:16, 0:16 * WA], T.CT[0:128:16, 0:16 * WA])),
                        [], [], dma=True, fixed=("rep", 16 * 15), after=(first,))
    zero_v(ZV[4])
    ts(whole("pX"), whole("xi"), -float(DEC), A.add)
    cp(whole("thf"), whole("thi"))
    ts(R("pi", 5, 6), whole("thi"), R("pf", 1, 2), A.add, -1.0, A.add)
    tt(whole("mx"), whole("pX"), R("d0", 0, V), A.max)
    spread_s(2)
    mm(whole("pX"), whole("Bm"), whole("mx"), True, True)
    convert("B", BW[0], BW[0] + BW[1])
    spread_s(1)
    ts(whole("ch"), whole("pX"), whole("thf"), A.is_ge)
    ts(whole("xa"), whole("mx"), 1.0 - DEC, A.add)
    scan(ff(0, V), whole("ch"), whole("line"), 0.0, A.add, A.max)
    ts(R("jf", 4, 5), R("pi", 1, 2), 16.0, A.mult)
    ts(whole("Im"), whole("mm"), R("pf", 0, 1), A.is_equal)
    for c in range(4 - SC):
        ts(R("cm", V * c, V * c + V), ff(0, V), R("jf", c, c + 1), A.is_le, 2.0, A.mult)
    spread_s(1)
    for c in range(4 - SC, 4):
        act(R("cm", V * c, V * c + V), ff(0, V), F.Sign, bias=R("jf", c, c + 1), scale=-1.0, accum_out=R("ea", 4 + c, 5 + c))
    together("v", (scan(R("GC", 128 * c, 128 * c + 128), R("cm", 256 * c, 256 * c + 128), R("cm", 256 * c + 128, 256 * c + 256),
                        -256.0, A.add, A.add) for c in range(8 - 2 * SC)))
    ts(R("pi", 6, 7), R("pi", 5, 6), 4, A.arith_shift_right)
    ts(whole("ku"), whole("ki"), R("jf", 4, 5), A.add)
    tt(R("ea", 4, 8 - SC), R("GC", 127, 1024 - 256 * SC, 256), R("GC", 255, 1024 - 256 * SC, 256), A.add)
    ts(R("pf", 6, 7), R("pi", 6, 7), -1.0, A.mult)
    spread_s(1)
    zero_v(ZV[3])
    listed(R("ea", 4, 8), 0.5, V / 2.0)
    send_ids(0)
    zero_g(ZG[1])
    convert("B", BW[0] + BW[1], WB)
    if NV:
        fill_v()
    spread_s(2)
    scaled = {0: ("F64", float(CAP)), 1: ("G64", -float(CAP)), 3: ("F33", float(SEG)), 5: ("NH", -1024.0 * SEG)}
    for i, c in enumerate(values(0)):
        if i in scaled and SK:
            act(whole(scaled[i][0]), whole("Im"), F.Copy, scale=scaled[i][1])
        elif i in scaled:
            ts(whole(scaled[i][0]), whole("mm"), R("pf", 0, 1), A.is_equal, scaled[i][1], A.mult)
    send_values(0)
    record("y", None, [], [], after=(cp(X(whole("Ls"), whole("U")), R("sm", 192, 256)),))
    load_fan(peers[FA:])
    rest = zend - zpos[0]
    if pending:
        spread_v()
    mine = lists(whole("U"), 64, "Eo", "Ho", "Uo", 0, "pX")
    for i, n in enumerate(NS):
        spread_s(n)
        if NV > i + 1:
            fill_v()
        if i == len(NS) - 1:
            spread_s(NL)
            for j in range(4):
                next(mine)
        zero_v(rest // len(NS) // 16 * 16 if i < len(NS) - 1 else zend - zpos[0])
        if pending:
            spread_v()
    spread_s(len(runs))
    for c in mine:
        pass
    ts(R("xb", 0, C0), R("d0", V, V + C0), 1.0, A.add)
    if SV:
        value_gather(whole("VO"), "Uo", 64, 0, OWN0[GV0], 0)
    else:
        cp(R("GV", 0, 16 * OWN0[GV0]), X(whole("VO"), R("Uo", 64, 64 + OWN0[GV0])))
    record("s", None, [], [], after=(copied,))
    tt(cells(1, 0, C0), R("xb", 0, C0), R("pS", 0, C0), A.mult)
    for a in range(0, V, PW):
        later = tt(cells(0, a, a + PW), R("xa", a, a + PW), R("pS", 0, PW), A.mult)
    load("y", R("dr", 0, V), T.drv[:, V:2 * V], after=(later,))
    items(0)
    load("y", R("dr", V, 3 * V), T.drv[:, 2 * V:RO * V], after=(len(ops) - 7,))
    scaled_drive(1)
    act(cells(1, C0, V), R("dS", C0, V), F.Copy)
    for name, src, k in (("NI", "Im", -1.0), ("TW", "Bm", R("pf", 6, 7)), ("NB", "Bm", -1.0), ("B2", "Bm", 2.0),
                         ("N16", "Im", -float(DEC))):
        act(whole(name), whole(src), F.Identity, scale=k)
    for h in (0, 256):
        scales("St", h)
        act(R("iS0", h, h + 256), whole("kf"), F.Exp, scale=-8 * LN2)

    def view(a, b):
        return R("SG", SEG * a + SEG - 1, SEG * b, SEG)

    def sums(a, b):
        return R("pR0", a, b) if a == 0 else R("pR0", 512 + a, 512 + b) if a < F1 else R("pS", a - F1, b - F1)

    def differ(a, b):
        summed(bank(0, a, b), ("NI", R("Ls", a, b)), ("Im", view(a, b)))

    def summed_abs(a, b):
        act(R("mx", a, b), bank(0, a, b), F.Abs)
        summed(sums(a, b), ("TW", R("St", a, b)), ("Bm", R("mx", a, b)))

    def mark(a, b):
        act(R("mx", a, b), sums(a, b), F.Sign)
        act(R("ch", a, b), R("mx", a, b), F.Relu)

    def count(a, b):
        scan(ff(a, b), R("ch", a, b), R("line", a, b), ff(a - 1, a) if a else 0.0, A.add, A.max)

    def before(c):
        act(R(("xa", "jk")[c % 2], 0, F0), ff(0, F0), F.Sign, bias=R("jf", c, c + 1), scale=-1.0, accum_out=R("ea", c, c + 1))

    def fallen(k, a, b):
        summed(bank(k, a, b), ("Im", view(a, b)), ("N16", R("St", a, b)))

    def fall_cells(k, a, b):
        act(cells(0, a, b), bank(k, a, b), F.Copy)

    def drive_cells(a, b):
        act(cells(1, a, b), R("dS", a, b), F.Copy)

    def last_sums():
        for a, b in ((F1, V - 16), (V - 16, V)):
            tt(R("mx", a, b), view(a, b), R("Ls", a, b), A.max)
        summed(sums(F1, V), ("TW", R("St", F1, V)), ("NB", R("Ls", F1, V)), ("NB", view(F1, V)), ("B2", R("mx", F1, V)))

    def last_marks(run, a):
        ts(R("ch", a, F1), sums(a, F1), 0.0, A.is_gt)
        run(a, F1)
        ts(R("ch", F1, V), sums(F1, V), 0.0, A.is_gt)
        run(F1, V)

    def choose():
        h = FW // 2
        for c in range(4):
            if c == 3:
                ts(R("ea", 4, 8), R("ea", 0, 4), 0.5, A.mult, F0 / 2.0 - 256, A.add)
            ts(R("cl", FW * c, FW * c + FW), ff(F0, V), R("jf", c, c + 1), A.is_le)
        together("v", (scan(R("xs", h * c, h * c + h), R("cl", FW * c, FW * c + h), R("cl", FW * c + h, FW * c + FW),
                            R("ea", 4 + c, 5 + c), A.add, A.add) for c in range(4)))
        listed(R("xs", h - 1, 4 * h, h), 1.0, 256.0)

    outs = []

    def kept(a, b):
        act(R("dd", a, b), bank(0, a, b), F.Copy)

    def capped(a, b):
        scan(ff(a, b), R("ch", a, b), R("c64", 0, b - a), ff(a - 1, a), A.add, A.min)

    def unscaled(name, first, step):
        together("t", (mm(R("pX", k, FL, 16), R("IK", 128 * k, 128 * k + 128),
                          R(name, first + step * k, step * FL, 16 * step), True, True) for k in range(16)))

    def old_last():
        unscaled("Ls", 0, 1)
        act(R("dS", 0, FL), R("pX", 0, FL), F.Copy)

    def first_x():
        unscaled("SG", SEG - 1, SEG)
        act(R("dd", 0, FL), R("pX", 0, FL), F.Identity, bias=-256.0)
        act(R("xo", 0, FL), R("pX", 0, FL), F.Identity, bias=-1.0)
        outs.append(store("y", T.yx[:, 0:FL], R("xo", 0, FL)))

    def gate():
        summed(bank(2, 0, FL), ("BI", ff(0, FL)), ("NBI", ff(-1, FL - 1)), ("Im", R("dd", 0, FL)))
        summed(bank(2, FL, 2 * FL), ("NBI", ff(0, FL)), ("BI", ff(-1, FL - 1)), ("Im", R("dS", 0, FL)))

    def first_last():
        act(R("cl", 0, 2 * FL), bank(2, 0, 2 * FL), F.Relu)
        summed(R("pR0", 0, FL), ("Im", R("cl", 0, FL)), ("Im", R("cl", FL, 2 * FL)))
        act(R("lo", 0, FL), R("pR0", 0, FL), F.Identity, bias=-1.0)
        outs.append(store("y", T.yl[:, 0:FL], R("lo", 0, FL)))

    def lowered(out, a, b):
        summed(out, ("Im", view(a, b)), ("NI", R("St", a, b)))

    def last_constants():
        act(whole("xb"), whole("iS0"), F.Copy, scale=2.0 ** 64)
        act(whole("c64"), R("line", 0, F0), F.Identity, bias=float(CAP), scale=0.0)
        act(ff(-1, 0), R("kf", 0, 1), F.Copy)
        for name, k in (("N64", -1.0 / CAP), ("BI", 256.0), ("NBI", -256.0)):
            act(whole(name), whole("Im"), F.Copy, scale=k)
        act(R("IK", 0, 128), whole("Im"), F.Copy, scale=2.0 ** 64)
        for n in (1, 2, 4, 8):
            act(R("IK", 128 * n, 256 * n), R("IK", 0, 128 * n), F.Copy, scale=2.0 ** (-8 * n))

    def do(*calls):
        return [(c[0], c[1:]) for c in calls]

    def scans(t, plan):
        stops = sorted(plan)
        for a in range(0, V, 16):
            name = ("scan", t, [n for n in stops if n > a][0])
            together("v", (scan(R("SG", SEG * a, SEG * (a + 16)), R("W", SEG * a, SEG * (a + 16)),
                                R("W", HALF + SEG * a, HALF + SEG * (a + 16)), 0.0, A.max, A.max) for j in (0,)), name)
            for fn, args in plan.get(a + 16, ()):
                fn(*args)

    for t in range(1, RO - 1):
        scaled_drive(t + 1)
        if t == RO - 2:
            last_constants()
        plan = {F0: do((differ, 0, F0), (fallen, 1, 0, F0), (drive_cells, 0, F0), (summed_abs, 0, F0), (fall_cells, 1, 0, F0),
                       (mark, 0, F0), (kept, 0, F0)),
                F1: do((differ, F0, F1), (summed_abs, F0, F1)),
                V - 16: [], V: do((last_sums,), (differ, F1, V), (fallen, 2, F0, V))}
        plan[CP] = plan.get(CP, []) + do((count, 0, F0), *[(before, c) for c in range(4)])
        scans(t, plan)
        last_marks(count, F0)
        choose()
        send_ids(t)
        kept(F0, V)
        fall_cells(2, F0, V)
        drive_cells(F0, V)
        own_lists(t)
        items(t)

    def stepped():
        summed(bank(3, 0, FL), ("Im", ff(0, FL)), ("NI", ff(-1, FL - 1)))

    def gated():
        tt(R("mx", 0, FL), bank(3, 0, FL), R("dd", 0, FL), A.mult)
        summed(R("pR0", 0, FL), ("Im", R("Ls", 0, FL)), ("NI", R("St", 0, FL)), ("Im", R("mx", 0, FL)))

    def out_l():
        tt(R("lo", 0, FL), R("pR0", 0, FL), R("xb", 0, FL), A.mult)
        outs.append(store("y", T.yl[:, 0:FL], R("lo", 0, FL)))

    def out_x():
        tt(R("xo", 0, FL), bank(2, 0, FL), R("xb", 0, FL), A.mult)
        outs.append(store("y", T.yx[:, 0:FL], R("xo", 0, FL)))

    if TAIL:
        old_last()
        scans(RO - 1, {FL: do((differ, 0, FL), (summed_abs, 0, FL), (mark, 0, FL), (first_x,)),
                       CL: do((capped, 0, FL), (gate,)),
                       F1: do((differ, FL, F1), (summed_abs, FL, F1), (lowered, bank(1, 0, F1 - FL), FL, F1), (first_last,)),
                       V - 16: [], V: do((last_sums,))})
    else:
        plan = {FL: do((differ, 0, FL), (lowered, bank(2, 0, FL), 0, FL), (summed_abs, 0, FL), (kept, 0, FL), (mark, 0, FL)),
                FL + 48: do((out_x,)),
                F1: do((differ, FL, F1), (summed_abs, FL, F1), (lowered, bank(2, 0, F1 - FL), FL, F1)),
                V - 16: do((gated,)), V: do((last_sums,), (out_l,))}
        plan[CL] = plan.get(CL, []) + do((capped, 0, FL), (stepped,))
        scans(RO - 1, plan)
    d_end, x_end = R("pX", 256, 256 + V - F1), R("pX", 384, 384 + V - F1)
    summed(d_end, ("NI", R("Ls", F1, V)), ("Im", view(F1, V)))
    lowered(x_end, F1, V)
    ts(R("ch", FL, F1), sums(FL, F1), 0.0, A.is_gt)
    tt(R("acc", FL, F1), bank(0, FL, F1), R("xb", FL, F1), A.mult)
    parts = ((3, FL, F1), (1, F1, V))
    for k, a, b in parts:
        if a == F1:
            ts(R("ch", F1, V), sums(F1, V), 0.0, A.is_gt)
            tt(R("xo", FL, F1), bank(1 if TAIL else 2, 0, F1 - FL), R("xb", FL, F1), A.mult)
        capped(a, b)
        summed(bank(k, a, b), ("N64", R("c64", 0, b - a)), ("Im", ff(a, b)), ("NI", ff(a - 1, b - 1)))
    tt(R("xo", F1, V), x_end, R("xb", F1, V), A.mult)
    outs.append(store("s", T.yx[:, FL:V], R("xo", FL, V)))
    tt(R("acc", F1, V), d_end, R("xb", F1, V), A.mult)
    for k, a, b in parts:
        tt(R("pX", a - FL, b - FL), bank(k, a, b), R("acc", a, b), A.mult)
    for k, a, b in parts:
        tt(R("lo", a, b), R("pX", a - FL, b - FL), R("xo", a, b), A.add)
    outs.append(store("y", T.yl[:, FL:V], R("lo", FL, V)))
    record("y", None, [], [], after=outs)

    known = {q: set() for q in Q}
    snap = {}
    members = {}
    for i, o in enumerate(ops):
        members.setdefault(o["group"], []).append(i)
    needed = set()
    for i, o in enumerate(ops):
        q = o["q"]
        if q is None:
            snap[i] = set()
            continue
        waits = []
        for d in sorted(o["deps"], reverse=True):
            if d not in known[q]:
                waits.append(d)
                known[q] |= snap[d] | {d}
                if not ops[d]["dma"]:
                    known[q] |= {j for j in range(d) if ops[j]["q"] == ops[d]["q"] and not ops[j]["dma"]}
                if ops[d]["fixed"] is not None:
                    known[q] |= {j for j in range(i) if ops[j]["fixed"] == ops[d]["fixed"]}
                if ops[d]["group"] is not None:
                    for j in members[ops[d]["group"]]:
                        known[q] |= snap[j] | {j}
                        needed.add(j)
        o["waits"] = waits
        needed.update(waits)
        snap[i] = set(known[q])
    event = {}
    pool = {q: [[q + str(k), 0, None] for k in range(POOL[q])] for q in POOL}
    turn = {q: 0 for q in POOL}
    waited = set()
    for i, o in enumerate(ops):
        q = o["q"]
        if o["fixed"] is not None:
            event[i] = o["fixed"]
        if q is None:
            continue
        for ev in sorted({event[d] for d in o["waits"]}):
            Q[q].wait_ge(T.sem[ev[0]], ev[1])
            waited.add(ev)
        if o["fn"] is None:
            continue
        ins = o["fn"]()
        inc = 16 if o["dma"] else 1
        if o["fixed"] is not None:
            if o["fixed"][0] == "rep":
                ins.then_inc(T.sem.rep, 16)
        elif i in event:
            ins.then_inc(T.sem[event[i][0]], inc)
        elif i in needed:
            n = len(pool[q])
            k = [(turn[q] + j) % n for j in range(n)
                 if pool[q][(turn[q] + j) % n][2] is None or pool[q][(turn[q] + j) % n][2] in snap[i]][0]
            turn[q] = k + 1
            mine = [i] if o["group"] is None else members[o["group"]]
            pool[q][k][1] += inc * len(mine)
            pool[q][k][2] = mine[-1]
            ins.then_inc(T.sem[pool[q][k][0]], inc)
            for j in mine:
                event[j] = (pool[q][k][0], pool[q][k][1])
    for ev in sorted({o["fixed"] for o in ops if o["fixed"] is not None} - waited):
        g.wait_ge(T.sem[ev[0]], ev[1])
